import numpy as np
import ml_dtypes


def mxq(x, axis, fmt="e4m3"):
    dtype, down = {"e4m3": (ml_dtypes.float8_e4m3fn, 7), "e5m2": (ml_dtypes.float8_e5m2, 14)}[fmt]
    v = np.moveaxis(np.asarray(x, np.float32).astype(ml_dtypes.bfloat16).astype(np.float64), axis, -1)
    blocks = v.reshape(v.shape[:-1] + (-1, 32))
    amax = np.abs(blocks).max(-1, keepdims=True)
    byte = np.maximum(np.where(amax > 0, np.frexp(amax)[1] - 1 + 127, 0) - down, 1)
    scale = np.exp2(byte - 127.0)
    codes = (blocks / scale).astype(np.float32).astype(dtype).astype(np.float64)
    return np.moveaxis((codes * scale).reshape(v.shape), -1, axis)


WIDE = False


def mx_kscale(k):
    if not WIDE:
        return np.ones(k)
    levels = np.array([10, -10, 5, -5, 0])
    if k % 512:
        return np.exp2(np.random.permutation(np.resize(levels, k // 32))).repeat(32)
    a = np.empty((k // 512, 16))
    for p in range(k // 512):
        a[p, :8] = np.random.permutation(np.resize(levels, 8))
        for g in range(8):
            far = levels[np.abs(levels - a[p, g]) >= 10]
            a[p, g + 8] = far[np.random.randint(len(far))]
    return np.exp2(a.ravel()).repeat(32)


def f64(x):
    return np.asarray(x).astype(np.float64)


E2M1 = np.array([0.0, 0.5, 1.0, 1.5, 2.0, 3.0, 4.0, 6.0, -0.0, -0.5, -1.0, -1.5, -2.0, -3.0, -4.0, -6.0])


def pack_weight(w, fmt):
    k, n = w.shape
    w = f64(np.asarray(w, np.float32).astype(ml_dtypes.bfloat16)).reshape(k // 32, 32, n)
    amax = np.abs(w).max(1)
    if fmt == "e4m3":
        byte = np.frexp(amax)[1] - 1 + 127 - 7
    else:
        mant, ex = np.frexp(amax / 6.0)
        byte = np.where(mant > 0.5, ex, ex - 1) + 127
    byte = np.clip(np.where(amax > 0, byte, 1), 1, 254)
    scaled = (w * np.exp2(127.0 - byte)[:, None, :]).reshape(k, n).astype(np.float32)
    by_word = np.ascontiguousarray(scaled.reshape(k // 512, 128, 4, n).transpose(0, 1, 3, 2))
    if fmt == "e4m3":
        words = by_word.astype(ml_dtypes.float8_e4m3fn).view(np.uint8)
    else:
        c = by_word.astype(ml_dtypes.float4_e2m1fn).view(np.uint8) & 0xF
        words = (c[..., 0::2] | (c[..., 1::2] << 4)).reshape(k // 512, 128, 2 * n)
    return np.ascontiguousarray(words), np.ascontiguousarray(byte.astype(np.uint8).reshape(k // 512, 16, n))


def unpack_weight(words, scales, fmt):
    g, _, n = scales.shape
    words = np.ascontiguousarray(words).reshape(g, 128, n, -1)
    if fmt == "e4m3":
        vals = words.view(ml_dtypes.float8_e4m3fn).astype(np.float64)
    else:
        nib = np.empty((g, 128, n, 4), np.uint8)
        nib[..., 0::2] = words & 0xF
        nib[..., 1::2] = words >> 4
        vals = E2M1[nib]
    vals = vals * np.repeat(np.exp2(scales.astype(np.float64) - 127.0), 8, axis=1)[..., None]
    return vals.transpose(0, 1, 3, 2).reshape(g * 512, n)


O, K, R, M, T = 1024, 2048, 512, 1536, 512


def setup_inputs():
    n = np.random.standard_normal
    s = mx_kscale(K)[:, None]
    u = mx_kscale(R)[:, None]
    x = n((K, T)); x[:O] *= 6.0
    w = n((K, M)) / np.sqrt(K) / s; w[:O] /= 2.0
    p_w8 = pack_weight(w[:O], "e4m3")
    p_w4 = pack_weight(w[O:], "e2m1")
    p_up = pack_weight(n((R, M)) / np.sqrt(R) / u, "e2m1")
    return {
        "x": (x * s).astype(np.float32),
        "w8_words": p_w8[0],
        "w8_scales": p_w8[1],
        "w4_words": p_w4[0],
        "w4_scales": p_w4[1],
        "down": (0.3 * n((K, R)) / np.sqrt(K) / s * u.T).astype(np.float32),
        "up_words": p_up[0],
        "up_scales": p_up[1],
    }


def reference(x, w8_words, w8_scales, w4_words, w4_scales, down, up_words, up_scales):
    x_ = mxq(f64(x), 0, "e4m3")
    w8_ = unpack_weight(w8_words, w8_scales, "e4m3")
    w4_ = unpack_weight(w4_words, w4_scales, "e2m1")
    down_ = mxq(f64(down), 0, "e4m3")
    up_ = unpack_weight(up_words, up_scales, "e2m1")
    h_ = mxq(down_.T @ x_, 0, "e4m3")
    y = w8_.T @ x_[:O] + w4_.T @ x_[O:] + up_.T @ h_
    return y

@@ -1,0 +1,216 @@
+from contextlib import ExitStack
+
+import concourse.mybir as mybir
+
+K, T, R, M = 2048, 512, 512, 1536
+FLOPS = 2 * (K * R * T + K * M * T + R * M * T)
+
+F32 = mybir.dt.float32
+BF16 = mybir.dt.bfloat16
+I32 = mybir.dt.int32
+U32 = mybir.dt.uint32
+U8 = mybir.dt.uint8
+FP8X4 = mybir.dt.float8_e4m3fn_x4
+FP4X4 = mybir.dt.float4_e2m1fn_x4
+
+P = 128
+PACK = 4
+G = 512
+X_VEC = 288
+D_VEC = 80
+H_VEC = 344
+
+
+def tile_mix_three_fm_none_kernel(
+    tc, x, w8_words, w8_scales, w4_words, w4_scales, down, up_words, up_scales, out
+):
+    nc = tc.nc
+    with ExitStack() as ctx:
+        keep = ctx.enter_context(tc.tile_pool(name="keep", bufs=1))
+        psum = ctx.enter_context(tc.psum_pool(name="psum", bufs=1))
+        ctx.enter_context(tc.manual_schedule())
+
+        def sb(name, shape, dtype):
+            return keep.tile(shape, dtype, name=name, align_bytes=256)
+
+        planes0 = sb("planes0", [P, 4, G], U8)
+        planes1 = sb("planes1", [P, 4, M - G], U8)
+        up_plane = sb("up_plane", [P, M], U8)
+        warm_in = sb("warm_in", [P, 1], F32)
+        warm_out = sb("warm_out", [P, 1], F32)
+        nc.vector.memset(planes0[:].rearrange("p a n -> p (a n)").bitcast(I32), 0)
+        nc.vector.memset(warm_in[:], 0.0)
+        nc.vector.memset(planes1[:].rearrange("p a n -> p (a n)").bitcast(I32), 0)
+        nc.vector.memset(up_plane[:].bitcast(I32), 0)
+        nc.scalar.copy(warm_out[:], warm_in[:])
+
+        w8_rows = w8_scales.rearrange("a (q r) n -> r q a n", r=4)
+        w4_rows = w4_scales.rearrange("a (q r) n -> r q a n", r=4)
+        up_rows = up_scales.rearrange("a (q r) n -> r q a n", r=4)
+
+        def load_scales(queue, plane, rows, r, cols):
+            queue.dma_start(out=plane[r:P:32].bitcast(I32), in_=rows[r][:, :, cols].bitcast(I32))
+
+        for r in range(4):
+            load_scales(nc.gpsimd, planes0[:, 0:2, :], w8_rows, r, slice(0, G))
+        for r in range(4):
+            load_scales(nc.gpsimd, planes0[:, 2:4, :], w4_rows, r, slice(0, G))
+
+        x_raw = [sb(f"x_raw{c}", [P, PACK, T], F32) for c in range(4)]
+        d_raw = [sb(f"d_raw{c}", [P, PACK, R], F32) for c in range(3)]
+        d_raw_half = [sb(f"d_rawh{i}", [P, 2, R], F32) for i in range(2)]
+        w8_t = [sb(f"w8_{g}", [P, 2, G], U32) for g in range(3)]
+        w4_t = [sb(f"w4_{g}", [P, 2, 2 * G], U8) for g in range(3)]
+        up_t = sb("up_t", [P, 2 * M], U8)
+        w8_view = w8_words.rearrange("a p n i -> p a (n i)")
+        w4_view = w4_words.rearrange("a p b -> p a b")
+
+        def load_k(tile, src, c, j0=0, j1=PACK):
+            rows = src[512 * c : 512 * (c + 1), :].rearrange("(p j) w -> p j w", j=PACK)
+            nc.sync.dma_start(out=tile[:], in_=rows[:, j0:j1, :])
+
+        def load_w(g):
+            nc.sync.dma_start(out=w8_t[g][:].bitcast(I32), in_=w8_view[:, :, 4 * G * g : 4 * G * (g + 1)].bitcast(I32))
+            nc.sync.dma_start(out=w4_t[g][:].bitcast(I32), in_=w4_view[:, :, 2 * G * g : 2 * G * (g + 1)].bitcast(I32))
+
+        load_k(x_raw[0], x, 0)
+        load_k(x_raw[1], x, 1)
+        load_k(x_raw[2], x, 2)
+        load_k(x_raw[3], x, 3)
+        load_w(0)
+        for c in range(3):
+            load_k(d_raw[c], down, c)
+        for i in range(2):
+            load_k(d_raw_half[i], down, 3, 2 * i, 2 * i + 2)
+        load_w(1)
+        for r in range(4):
+            load_scales(nc.sync, planes1[:, 0:2, :], w8_rows, r, slice(G, M))
+        for r in range(4):
+            load_scales(nc.sync, planes1[:, 2:4, :], w4_rows, r, slice(G, M))
+        nc.sync.dma_start(out=up_t[:].bitcast(I32), in_=up_words[0].bitcast(I32))
+        for r in range(4):
+            nc.sync.dma_start(out=up_plane[r:P:32, :].bitcast(I32), in_=up_rows[r][:, 0, :].bitcast(I32))
+        load_w(2)
+
+        x_q = [sb(f"x_q{c}", [P, T], U32) for c in range(4)]
+        x_s = [sb(f"x_s{c}", [P, T], U8) for c in range(4)]
+        x_b = [sb(f"x_b{c}", [P, PACK * T], BF16) for c in range(4)]
+
+        def interleave(copy, dst, raw, a, b):
+            copy(
+                dst[:, PACK * a : PACK * b].rearrange("p (c i t) -> p c t i", i=4, t=4),
+                raw[:, :, a:b].rearrange("p t (c i) -> p c t i", i=4),
+            )
+
+        for c in range(4):
+            interleave(nc.vector.tensor_copy, x_b[c], x_raw[c], 0, X_VEC)
+            interleave(nc.scalar.copy, x_b[c], x_raw[c], X_VEC, T)
+            nc.vector.quantize_mx(out=x_q[c][:].bitcast(FP8X4), scales=x_s[c][:], in_=x_b[c][:])
+
+        def bank(i):
+            return psum.tile([P, T], F32, name=f"bank{i}")
+
+        acc = {}
+
+        def w_pass(i, c, tile=None, cols=slice(0, T)):
+            g, n = divmod(i, 4)
+            tile = acc[i] if tile is None else tile
+            if c < 2:
+                lhs = w8_t[g][:, c, P * n : P * (n + 1)].bitcast(FP8X4)
+            else:
+                lhs = w4_t[g][:, c - 2, 2 * P * n : 2 * P * (n + 1)].bitcast(FP4X4)
+            if g == 0:
+                lhs_scale = planes0[:, c, P * n : P * (n + 1)]
+            else:
+                lhs_scale = planes1[:, c, P * i - G : P * (i + 1) - G]
+            nc.tensor.matmul_mx(
+                out=tile[:], lhsT=lhs, lhsT_scale=lhs_scale,
+                rhs=x_q[c][:, cols].bitcast(FP8X4), rhs_scale=x_s[c][:, cols], start=(c == 0), stop=False,
+            )
+
+        for i in range(4):
+            acc[i] = bank(i)
+        for c in range(2):
+            for i in range(4):
+                w_pass(i, c)
+
+        d_q = [sb(f"d_q{c}", [P, R], U32) for c in range(4)]
+        d_s = [sb(f"d_s{c}", [P, R], U8) for c in range(4)]
+        d_b = [sb(f"d_b{c}", [P, PACK * R], BF16) for c in range(4)]
+        h_acc = [bank(4 + t) for t in range(4)]
+
+        def permute(copy, dst, raw, a, b, j0=0, j1=PACK):
+            copy(
+                dst[:].rearrange("p (t m j) -> p m j t", t=4, j=4)[:, a:b, j0:j1],
+                raw[:].rearrange("p j (m t) -> p m j t", t=4)[:, a:b],
+            )
+
+        def h_pass(t, c):
+            cols = slice(P * t, P * (t + 1))
+            nc.tensor.matmul_mx(
+                out=h_acc[t][:], lhsT=d_q[c][:, cols].bitcast(FP8X4), lhsT_scale=d_s[c][:, cols],
+                rhs=x_q[c][:].bitcast(FP8X4), rhs_scale=x_s[c][:], start=(c == 0), stop=(c == 3),
+            )
+
+        for c in range(3):
+            permute(nc.vector.tensor_copy, d_b[c], d_raw[c], 0, D_VEC)
+            permute(nc.scalar.copy, d_b[c], d_raw[c], D_VEC, P)
+            nc.vector.quantize_mx(out=d_q[c][:].bitcast(FP8X4), scales=d_s[c][:], in_=d_b[c][:])
+            for t in range(4):
+                h_pass(t, c)
+            if c < 2:
+                for i in range(4):
+                    w_pass(i, c + 2)
+        for i in range(2):
+            permute(nc.vector.tensor_copy, d_b[3], d_raw_half[i], 0, D_VEC, 2 * i, 2 * i + 2)
+            permute(nc.scalar.copy, d_b[3], d_raw_half[i], D_VEC, P, 2 * i, 2 * i + 2)
+        for t in range(4):
+            cols = slice(P * t, P * (t + 1))
+            nc.vector.quantize_mx(
+                out=d_q[3][:, cols].bitcast(FP8X4), scales=d_s[3][:, cols],
+                in_=d_b[3][:, 512 * t : 512 * (t + 1)],
+            )
+            h_pass(t, 3)
+
+        h_t = sb("h_t", [P, PACK, T], BF16)
+        h_b = sb("h_b", [P, PACK * T], BF16)
+        h_q = sb("h_q", [P, T], U32)
+        h_s = sb("h_s", [P, T], U8)
+        for t in range(4):
+            copy = nc.vector.tensor_copy if t % 2 else nc.scalar.copy
+            copy(h_t[:, t, :], h_acc[t][:])
+        interleave(nc.vector.tensor_copy, h_b, h_t, 0, H_VEC)
+        interleave(nc.scalar.copy, h_b, h_t, H_VEC, T)
+        nc.vector.quantize_mx(out=h_q[:].bitcast(FP8X4), scales=h_s[:], in_=h_b[:])
+
+        def up_pass(i, tile=None, cols=slice(0, T), on_scalar=None):
+            tile = acc[i] if tile is None else tile
+            on_scalar = i % 2 if on_scalar is None else on_scalar
+            nc.tensor.matmul_mx(
+                out=tile[:], lhsT=up_t[:, 2 * P * i : 2 * P * (i + 1)].bitcast(FP4X4),
+                lhsT_scale=up_plane[:, P * i : P * (i + 1)],
+                rhs=h_q[:, cols].bitcast(FP8X4), rhs_scale=h_s[:, cols], start=False, stop=True,
+            )
+            res = sb(f"res{i}_{cols.start}", [P, cols.stop - cols.start], F32)
+            copy = nc.scalar.copy if on_scalar else nc.vector.tensor_copy
+            copy(res[:], tile[:])
+            nc.sync.dma_start(out=out[P * i : P * (i + 1), cols], in_=res[:])
+
+        for i in range(4, 8):
+            acc[i] = bank(i)
+        for c in range(4):
+            for i in range(4, 8):
+                w_pass(i, c)
+        for i in range(8):
+            up_pass(i)
+        for i in range(8, 11):
+            acc[i] = bank(i - 8)
+            for c in range(4):
+                w_pass(i, c)
+            up_pass(i)
+        for q in range(4):
+            cols = slice(P * q, P * (q + 1))
+            tile = psum.tile([P, P], F32, name=f"bank{3 + q}")
+            for c in range(4):
+                w_pass(11, c, tile, cols)
+            up_pass(11, tile, cols, q % 2)

@@ -15,10 +15,10 @@ FP4X4 = mybir.dt.float4_e2m1fn_x4
 
 P = 128
 PACK = 4
-G = 512
-X_VEC = 288
-D_VEC = 80
-H_VEC = 344
+EARLY = 1024
+W8_ROW = 4
+X_VEC = 320
+D_VEC = 84
 
 
 def tile_mix_three_fm_none_kernel(
@@ -33,14 +33,14 @@ def tile_mix_three_fm_none_kernel(
         def sb(name, shape, dtype):
             return keep.tile(shape, dtype, name=name, align_bytes=256)
 
-        planes0 = sb("planes0", [P, 4, G], U8)
-        planes1 = sb("planes1", [P, 4, M - G], U8)
+        w4_plane = sb("w4_plane", [P, 2, M], U8)
+        w8_plane = sb("w8_plane", [P, 2, M], U8)
         up_plane = sb("up_plane", [P, M], U8)
         warm_in = sb("warm_in", [P, 1], F32)
         warm_out = sb("warm_out", [P, 1], F32)
-        nc.vector.memset(planes0[:].rearrange("p a n -> p (a n)").bitcast(I32), 0)
+        nc.vector.memset(w4_plane[:].rearrange("p a n -> p (a n)").bitcast(I32), 0)
         nc.vector.memset(warm_in[:], 0.0)
-        nc.vector.memset(planes1[:].rearrange("p a n -> p (a n)").bitcast(I32), 0)
+        nc.vector.memset(w8_plane[:].rearrange("p a n -> p (a n)").bitcast(I32), 0)
         nc.vector.memset(up_plane[:].bitcast(I32), 0)
         nc.scalar.copy(warm_out[:], warm_in[:])
 
@@ -48,19 +48,21 @@ def tile_mix_three_fm_none_kernel(
         w4_rows = w4_scales.rearrange("a (q r) n -> r q a n", r=4)
         up_rows = up_scales.rearrange("a (q r) n -> r q a n", r=4)
 
-        def load_scales(queue, plane, rows, r, cols):
-            queue.dma_start(out=plane[r:P:32].bitcast(I32), in_=rows[r][:, :, cols].bitcast(I32))
+        def load_w4_scales():
+            for r in range(4):
+                nc.sync.dma_start(out=w4_plane[r:P:32].bitcast(I32), in_=w4_rows[r].bitcast(I32))
 
-        for r in range(4):
-            load_scales(nc.gpsimd, planes0[:, 0:2, :], w8_rows, r, slice(0, G))
-        for r in range(4):
-            load_scales(nc.gpsimd, planes0[:, 2:4, :], w4_rows, r, slice(0, G))
+        def load_w8_scales():
+            for r in range(4):
+                nc.sync.dma_start(out=w8_plane[W8_ROW + r : P : 32].bitcast(I32), in_=w8_rows[r].bitcast(I32))
 
         x_raw = [sb(f"x_raw{c}", [P, PACK, T], F32) for c in range(4)]
         d_raw = [sb(f"d_raw{c}", [P, PACK, R], F32) for c in range(3)]
         d_raw_half = [sb(f"d_rawh{i}", [P, 2, R], F32) for i in range(2)]
-        w8_t = [sb(f"w8_{g}", [P, 2, G], U32) for g in range(3)]
-        w4_t = [sb(f"w4_{g}", [P, 2, 2 * G], U8) for g in range(3)]
+        w8_early = [sb(f"w8_early{a}", [P, EARLY], U32) for a in range(2)]
+        w4_early = sb("w4_early", [P, 2, 2 * EARLY], U8)
+        w8_late = sb("w8_late", [P, 2, M - EARLY], U32)
+        w4_late = sb("w4_late", [P, 2, 2 * (M - EARLY)], U8)
         up_t = sb("up_t", [P, 2 * M], U8)
         w8_view = w8_words.rearrange("a p n i -> p a (n i)")
         w4_view = w4_words.rearrange("a p b -> p a b")
@@ -69,28 +71,27 @@ def tile_mix_three_fm_none_kernel(
             rows = src[512 * c : 512 * (c + 1), :].rearrange("(p j) w -> p j w", j=PACK)
             nc.sync.dma_start(out=tile[:], in_=rows[:, j0:j1, :])
 
-        def load_w(g):
-            nc.sync.dma_start(out=w8_t[g][:].bitcast(I32), in_=w8_view[:, :, 4 * G * g : 4 * G * (g + 1)].bitcast(I32))
-            nc.sync.dma_start(out=w4_t[g][:].bitcast(I32), in_=w4_view[:, :, 2 * G * g : 2 * G * (g + 1)].bitcast(I32))
+        def load_bytes(tile, src):
+            nc.sync.dma_start(out=tile[:].bitcast(I32), in_=src.bitcast(I32))
 
-        load_k(x_raw[0], x, 0)
-        load_k(x_raw[1], x, 1)
         load_k(x_raw[2], x, 2)
+        load_w4_scales()
+        load_bytes(w4_early, w4_view[:, :, : 2 * EARLY])
         load_k(x_raw[3], x, 3)
-        load_w(0)
+        load_k(x_raw[0], x, 0)
+        load_w8_scales()
+        load_bytes(w8_early[0], w8_view[:, 0, : 4 * EARLY])
+        load_k(x_raw[1], x, 1)
+        load_bytes(w8_early[1], w8_view[:, 1, : 4 * EARLY])
         for c in range(3):
             load_k(d_raw[c], down, c)
         for i in range(2):
             load_k(d_raw_half[i], down, 3, 2 * i, 2 * i + 2)
-        load_w(1)
-        for r in range(4):
-            load_scales(nc.sync, planes1[:, 0:2, :], w8_rows, r, slice(G, M))
-        for r in range(4):
-            load_scales(nc.sync, planes1[:, 2:4, :], w4_rows, r, slice(G, M))
-        nc.sync.dma_start(out=up_t[:].bitcast(I32), in_=up_words[0].bitcast(I32))
+        load_bytes(w8_late, w8_view[:, :, 4 * EARLY :])
+        load_bytes(w4_late, w4_view[:, :, 2 * EARLY :])
         for r in range(4):
             nc.sync.dma_start(out=up_plane[r:P:32, :].bitcast(I32), in_=up_rows[r][:, 0, :].bitcast(I32))
-        load_w(2)
+        load_bytes(up_t, up_words[0])
 
         x_q = [sb(f"x_q{c}", [P, T], U32) for c in range(4)]
         x_s = [sb(f"x_s{c}", [P, T], U8) for c in range(4)]
@@ -102,42 +103,45 @@ def tile_mix_three_fm_none_kernel(
                 raw[:, :, a:b].rearrange("p t (c i) -> p c t i", i=4),
             )
 
-        for c in range(4):
-            interleave(nc.vector.tensor_copy, x_b[c], x_raw[c], 0, X_VEC)
-            interleave(nc.scalar.copy, x_b[c], x_raw[c], X_VEC, T)
-            nc.vector.quantize_mx(out=x_q[c][:].bitcast(FP8X4), scales=x_s[c][:], in_=x_b[c][:])
-
-        def bank(i):
-            return psum.tile([P, T], F32, name=f"bank{i}")
+        def bank(b, shape):
+            return psum.tile(shape, F32, name=f"bank{b}")
 
         acc = {}
 
-        def w_pass(i, c, tile=None, cols=slice(0, T)):
-            g, n = divmod(i, 4)
-            tile = acc[i] if tile is None else tile
+        def w_pass(i, c, start, stop):
+            early = P * i < EARLY
+            n = i if early else i - EARLY // P
             if c < 2:
-                lhs = w8_t[g][:, c, P * n : P * (n + 1)].bitcast(FP8X4)
+                words = w8_early[c][:] if early else w8_late[:, c, :]
+                lhs = words[:, P * n : P * (n + 1)].bitcast(FP8X4)
+                lhs_scale = w8_plane[W8_ROW:P, c, P * i : P * (i + 1)]
             else:
-                lhs = w4_t[g][:, c - 2, 2 * P * n : 2 * P * (n + 1)].bitcast(FP4X4)
-            if g == 0:
-                lhs_scale = planes0[:, c, P * n : P * (n + 1)]
-            else:
-                lhs_scale = planes1[:, c, P * i - G : P * (i + 1) - G]
+                words = w4_early if early else w4_late
+                lhs = words[:, c - 2, 2 * P * n : 2 * P * (n + 1)].bitcast(FP4X4)
+                lhs_scale = w4_plane[:, c - 2, P * i : P * (i + 1)]
             nc.tensor.matmul_mx(
-                out=tile[:], lhsT=lhs, lhsT_scale=lhs_scale,
-                rhs=x_q[c][:, cols].bitcast(FP8X4), rhs_scale=x_s[c][:, cols], start=(c == 0), stop=False,
+                out=acc[i][:], lhsT=lhs, lhsT_scale=lhs_scale,
+                rhs=x_q[c][:].bitcast(FP8X4), rhs_scale=x_s[c][:], start=start, stop=stop,
             )
 
+        for i in range(8):
+            acc[i] = bank(i, [P, T])
+        for c in (2, 3, 0, 1):
+            interleave(nc.vector.tensor_copy, x_b[c], x_raw[c], 0, X_VEC)
+            interleave(nc.scalar.copy, x_b[c], x_raw[c], X_VEC, T)
+            nc.vector.quantize_mx(out=x_q[c][:].bitcast(FP8X4), scales=x_s[c][:], in_=x_b[c][:])
+            for i in range(8):
+                w_pass(i, c, c == 2, c == 1 and i < 4)
+
+        part = [sb(f"part{i}", [P, T], F32) for i in range(4)]
         for i in range(4):
-            acc[i] = bank(i)
-        for c in range(2):
-            for i in range(4):
-                w_pass(i, c)
+            copy = nc.vector.tensor_copy if i % 2 else nc.scalar.copy
+            copy(part[i][:], acc[i][:])
 
         d_q = [sb(f"d_q{c}", [P, R], U32) for c in range(4)]
         d_s = [sb(f"d_s{c}", [P, R], U8) for c in range(4)]
         d_b = [sb(f"d_b{c}", [P, PACK * R], BF16) for c in range(4)]
-        h_acc = [bank(4 + t) for t in range(4)]
+        h_acc = [bank(q, [P, PACK, P]) for q in range(4)]
 
         def permute(copy, dst, raw, a, b, j0=0, j1=PACK):
             copy(
@@ -145,11 +149,13 @@ def tile_mix_three_fm_none_kernel(
                 raw[:].rearrange("p j (m t) -> p m j t", t=4)[:, a:b],
             )
 
-        def h_pass(t, c):
-            cols = slice(P * t, P * (t + 1))
+        def h_pass(t, q, c):
+            rows = slice(P * t, P * (t + 1))
+            cols = slice(P * q, P * (q + 1))
             nc.tensor.matmul_mx(
-                out=h_acc[t][:], lhsT=d_q[c][:, cols].bitcast(FP8X4), lhsT_scale=d_s[c][:, cols],
-                rhs=x_q[c][:].bitcast(FP8X4), rhs_scale=x_s[c][:], start=(c == 0), stop=(c == 3),
+                out=h_acc[q][:, t, :], lhsT=d_q[c][:, rows].bitcast(FP8X4), lhsT_scale=d_s[c][:, rows],
+                rhs=x_q[c][:, cols].bitcast(FP8X4), rhs_scale=x_s[c][:, cols],
+                start=(c == 0 and t == 0), stop=(c == 3 and t == 3),
             )
 
         for c in range(3):
@@ -157,60 +163,79 @@ def tile_mix_three_fm_none_kernel(
             permute(nc.scalar.copy, d_b[c], d_raw[c], D_VEC, P)
             nc.vector.quantize_mx(out=d_q[c][:].bitcast(FP8X4), scales=d_s[c][:], in_=d_b[c][:])
             for t in range(4):
-                h_pass(t, c)
-            if c < 2:
-                for i in range(4):
-                    w_pass(i, c + 2)
+                for q in range(4):
+                    h_pass(t, q, c)
         for i in range(2):
             permute(nc.vector.tensor_copy, d_b[3], d_raw_half[i], 0, D_VEC, 2 * i, 2 * i + 2)
             permute(nc.scalar.copy, d_b[3], d_raw_half[i], D_VEC, P, 2 * i, 2 * i + 2)
         for t in range(4):
-            cols = slice(P * t, P * (t + 1))
+            rows = slice(P * t, P * (t + 1))
             nc.vector.quantize_mx(
-                out=d_q[3][:, cols].bitcast(FP8X4), scales=d_s[3][:, cols],
+                out=d_q[3][:, rows].bitcast(FP8X4), scales=d_s[3][:, rows],
                 in_=d_b[3][:, 512 * t : 512 * (t + 1)],
             )
-            h_pass(t, 3)
+            h_pass(t, 0, 3)
+            h_pass(t, 1, 3)
+        for q in (2, 3):
+            for t in range(4):
+                h_pass(t, q, 3)
 
-        h_t = sb("h_t", [P, PACK, T], BF16)
         h_b = sb("h_b", [P, PACK * T], BF16)
         h_q = sb("h_q", [P, T], U32)
         h_s = sb("h_s", [P, T], U8)
-        for t in range(4):
-            copy = nc.vector.tensor_copy if t % 2 else nc.scalar.copy
-            copy(h_t[:, t, :], h_acc[t][:])
-        interleave(nc.vector.tensor_copy, h_b, h_t, 0, H_VEC)
-        interleave(nc.scalar.copy, h_b, h_t, H_VEC, T)
-        nc.vector.quantize_mx(out=h_q[:].bitcast(FP8X4), scales=h_s[:], in_=h_b[:])
 
-        def up_pass(i, tile=None, cols=slice(0, T), on_scalar=None):
-            tile = acc[i] if tile is None else tile
-            on_scalar = i % 2 if on_scalar is None else on_scalar
-            nc.tensor.matmul_mx(
-                out=tile[:], lhsT=up_t[:, 2 * P * i : 2 * P * (i + 1)].bitcast(FP4X4),
-                lhsT_scale=up_plane[:, P * i : P * (i + 1)],
-                rhs=h_q[:, cols].bitcast(FP8X4), rhs_scale=h_s[:, cols], start=False, stop=True,
+        def h_out(copy, q):
+            copy(
+                h_b[:, 512 * q : 512 * (q + 1)].rearrange("p (n t) -> p n t", t=4),
+                h_acc[q][:].rearrange("p t n -> p n t"),
             )
-            res = sb(f"res{i}_{cols.start}", [P, cols.stop - cols.start], F32)
-            copy = nc.scalar.copy if on_scalar else nc.vector.tensor_copy
-            copy(res[:], tile[:])
-            nc.sync.dma_start(out=out[P * i : P * (i + 1), cols], in_=res[:])
 
+        def h_quantize(q0, q1):
+            cols = slice(P * q0, P * q1)
+            nc.vector.quantize_mx(
+                out=h_q[:, cols].bitcast(FP8X4), scales=h_s[:, cols], in_=h_b[:, 512 * q0 : 512 * q1]
+            )
+
+        h_out(nc.scalar.copy, 0)
+        h_out(nc.vector.tensor_copy, 1)
+        h_out(nc.scalar.copy, 2)
+        h_quantize(0, 1)
+        h_out(nc.vector.tensor_copy, 3)
+        h_quantize(1, 3)
+        h_quantize(3, 4)
+
+        def w_late(i):
+            acc[i] = bank(i - 8, [P, T])
+            for c in range(4):
+                w_pass(i, c, c == 0, False)
+
+        def finish(i, on_scalar=False):
+            if i < 4:
+                acc[i] = bank(4 + i, [P, T])
+            nc.tensor.matmul_mx(
+                out=acc[i][:], lhsT=up_t[:, 2 * P * i : 2 * P * (i + 1)].bitcast(FP4X4),
+                lhsT_scale=up_plane[:, P * i : P * (i + 1)],
+                rhs=h_q[:].bitcast(FP8X4), rhs_scale=h_s[:], start=(i < 4), stop=True,
+            )
+            res = sb(f"res{i}", [P, T], F32)
+            if i < 4:
+                nc.vector.tensor_add(res[:], acc[i][:], part[i][:])
+            elif on_scalar:
+                nc.scalar.copy(res[:], acc[i][:])
+            else:
+                nc.vector.tensor_copy(res[:], acc[i][:])
+            nc.sync.dma_start(out=out[P * i : P * (i + 1), :], in_=res[:])
+
+        w_late(8)
         for i in range(4, 8):
-            acc[i] = bank(i)
-        for c in range(4):
-            for i in range(4, 8):
-                w_pass(i, c)
-        for i in range(8):
-            up_pass(i)
-        for i in range(8, 11):
-            acc[i] = bank(i - 8)
-            for c in range(4):
-                w_pass(i, c)
-            up_pass(i)
-        for q in range(4):
-            cols = slice(P * q, P * (q + 1))
-            tile = psum.tile([P, P], F32, name=f"bank{3 + q}")
-            for c in range(4):
-                w_pass(11, c, tile, cols)
-            up_pass(11, tile, cols, q % 2)
+            finish(i, i % 2 == 0)
+        finish(8, True)
+        finish(0)
+        finish(1)
+        w_late(9)
+        finish(9, True)
+        finish(2)
+        finish(3)
+        for i in (10, 11):
+            w_late(i)
+            finish(i, True)

@@ -50,11 +50,11 @@ def tile_mix_three_fm_none_kernel(
 
         def load_w4_scales():
             for r in range(4):
-                nc.sync.dma_start(out=w4_plane[r:P:32].bitcast(I32), in_=w4_rows[r].bitcast(I32))
+                nc.gpsimd.dma_start(out=w4_plane[r:P:32].bitcast(I32), in_=w4_rows[r].bitcast(I32))
 
         def load_w8_scales():
             for r in range(4):
-                nc.sync.dma_start(out=w8_plane[W8_ROW + r : P : 32].bitcast(I32), in_=w8_rows[r].bitcast(I32))
+                nc.gpsimd.dma_start(out=w8_plane[W8_ROW + r : P : 32].bitcast(I32), in_=w8_rows[r].bitcast(I32))
 
         x_raw = [sb(f"x_raw{c}", [P, PACK, T], F32) for c in range(4)]
         d_raw = [sb(f"d_raw{c}", [P, PACK, R], F32) for c in range(3)]

@@ -38,10 +38,9 @@ def tile_mix_three_fm_none_kernel(
         up_plane = sb("up_plane", [P, M], U8)
         warm_in = sb("warm_in", [P, 1], F32)
         warm_out = sb("warm_out", [P, 1], F32)
-        nc.vector.memset(w4_plane[:].rearrange("p a n -> p (a n)").bitcast(I32), 0)
         nc.vector.memset(warm_in[:], 0.0)
+        nc.vector.memset(w4_plane[:].rearrange("p a n -> p (a n)").bitcast(I32), 0)
         nc.vector.memset(w8_plane[:].rearrange("p a n -> p (a n)").bitcast(I32), 0)
-        nc.vector.memset(up_plane[:].bitcast(I32), 0)
         nc.scalar.copy(warm_out[:], warm_in[:])
 
         w8_rows = w8_scales.rearrange("a (q r) n -> r q a n", r=4)
@@ -74,24 +73,20 @@ def tile_mix_three_fm_none_kernel(
         def load_bytes(tile, src):
             nc.sync.dma_start(out=tile[:].bitcast(I32), in_=src.bitcast(I32))
 
-        load_k(x_raw[2], x, 2)
-        load_w4_scales()
         load_bytes(w4_early, w4_view[:, :, : 2 * EARLY])
-        load_k(x_raw[3], x, 3)
-        load_k(x_raw[0], x, 0)
-        load_w8_scales()
+        load_w4_scales()
         load_bytes(w8_early[0], w8_view[:, 0, : 4 * EARLY])
-        load_k(x_raw[1], x, 1)
+        load_k(x_raw[2], x, 2)
+        load_k(x_raw[3], x, 3)
+        load_w8_scales()
         load_bytes(w8_early[1], w8_view[:, 1, : 4 * EARLY])
+        load_k(x_raw[0], x, 0)
+        load_k(x_raw[1], x, 1)
         for c in range(3):
             load_k(d_raw[c], down, c)
         for i in range(2):
             load_k(d_raw_half[i], down, 3, 2 * i, 2 * i + 2)
         load_bytes(w8_late, w8_view[:, :, 4 * EARLY :])
-        load_bytes(w4_late, w4_view[:, :, 2 * EARLY :])
-        for r in range(4):
-            nc.sync.dma_start(out=up_plane[r:P:32, :].bitcast(I32), in_=up_rows[r][:, 0, :].bitcast(I32))
-        load_bytes(up_t, up_words[0])
 
         x_q = [sb(f"x_q{c}", [P, T], U32) for c in range(4)]
         x_s = [sb(f"x_s{c}", [P, T], U8) for c in range(4)]
@@ -133,15 +128,18 @@ def tile_mix_three_fm_none_kernel(
             for i in range(8):
                 w_pass(i, c, c == 2, c == 1 and i < 4)
 
+        nc.vector.memset(up_plane[:].bitcast(I32), 0)
+        for r in range(4):
+            nc.sync.dma_start(out=up_plane[r:P:32, :].bitcast(I32), in_=up_rows[r][:, 0, :].bitcast(I32))
+        load_bytes(up_t, up_words[0])
+        load_bytes(w4_late, w4_view[:, :, 2 * EARLY :])
+
         part = [sb(f"part{i}", [P, T], F32) for i in range(4)]
-        for i in range(4):
-            copy = nc.vector.tensor_copy if i % 2 else nc.scalar.copy
-            copy(part[i][:], acc[i][:])
 
         d_q = [sb(f"d_q{c}", [P, R], U32) for c in range(4)]
         d_s = [sb(f"d_s{c}", [P, R], U8) for c in range(4)]
         d_b = [sb(f"d_b{c}", [P, PACK * R], BF16) for c in range(4)]
-        h_acc = [bank(q, [P, PACK, P]) for q in range(4)]
+        h_acc = []
 
         def permute(copy, dst, raw, a, b, j0=0, j1=PACK):
             copy(
@@ -162,6 +160,11 @@ def tile_mix_three_fm_none_kernel(
             permute(nc.vector.tensor_copy, d_b[c], d_raw[c], 0, D_VEC)
             permute(nc.scalar.copy, d_b[c], d_raw[c], D_VEC, P)
             nc.vector.quantize_mx(out=d_q[c][:].bitcast(FP8X4), scales=d_s[c][:], in_=d_b[c][:])
+            if c == 0:
+                for i in range(4):
+                    copy = nc.vector.tensor_copy if i == 3 else nc.scalar.copy
+                    copy(part[i][:], acc[i][:])
+                    h_acc.append(bank(i, [P, PACK, P]))
             for t in range(4):
                 for q in range(4):
                     h_pass(t, q, c)
@@ -204,9 +207,10 @@ def tile_mix_three_fm_none_kernel(
         h_quantize(1, 3)
         h_quantize(3, 4)
 
-        def w_late(i):
-            acc[i] = bank(i - 8, [P, T])
-            for c in range(4):
+        def w_late(i, passes):
+            if 0 in passes:
+                acc[i] = bank(i - 8, [P, T])
+            for c in passes:
                 w_pass(i, c, c == 0, False)
 
         def finish(i, on_scalar=False):
@@ -226,16 +230,15 @@ def tile_mix_three_fm_none_kernel(
                 nc.vector.tensor_copy(res[:], acc[i][:])
             nc.sync.dma_start(out=out[P * i : P * (i + 1), :], in_=res[:])
 
-        w_late(8)
+        w_late(8, (0, 1))
+        w_late(9, (0, 1))
         for i in range(4, 8):
             finish(i, i % 2 == 0)
-        finish(8, True)
-        finish(0)
-        finish(1)
-        w_late(9)
-        finish(9, True)
-        finish(2)
-        finish(3)
+        for i in (8, 9):
+            w_late(i, (2, 3))
+            finish(i, True)
+            finish(2 * (i - 8))
+            finish(2 * (i - 8) + 1)
         for i in (10, 11):
-            w_late(i)
+            w_late(i, (0, 1, 2, 3))
             finish(i, True)

@@ -15,10 +15,11 @@ FP4X4 = mybir.dt.float4_e2m1fn_x4
 
 P = 128
 PACK = 4
-EARLY = 1024
+G = 512
 W8_ROW = 4
 X_VEC = 320
 D_VEC = 84
+HALF_VEC = 164
 
 
 def tile_mix_three_fm_none_kernel(
@@ -55,42 +56,46 @@ def tile_mix_three_fm_none_kernel(
             for r in range(4):
                 nc.gpsimd.dma_start(out=w8_plane[W8_ROW + r : P : 32].bitcast(I32), in_=w8_rows[r].bitcast(I32))
 
-        x_raw = [sb(f"x_raw{c}", [P, PACK, T], F32) for c in range(4)]
-        d_raw = [sb(f"d_raw{c}", [P, PACK, R], F32) for c in range(3)]
-        d_raw_half = [sb(f"d_rawh{i}", [P, 2, R], F32) for i in range(2)]
-        w8_early = [sb(f"w8_early{a}", [P, EARLY], U32) for a in range(2)]
-        w4_early = sb("w4_early", [P, 2, 2 * EARLY], U8)
-        w8_late = sb("w8_late", [P, 2, M - EARLY], U32)
-        w4_late = sb("w4_late", [P, 2, 2 * (M - EARLY)], U8)
+        x_raw = {c: sb(f"x_raw{c}", [P, PACK, T], F32) for c in (2, 3, 0)}
+        x_raw_half = [sb(f"x_raw1_{h}", [P, PACK, T // 2], F32) for h in range(2)]
+        d_raw = [sb(f"d_raw{c}", [P, PACK, R], F32) for c in range(4)]
+        w4_t = sb("w4_t", [P, 2, 2 * M], U8)
+        w8_first = sb("w8_first", [P, 2 * G], U32)
+        w8_second = [sb(f"w8_second{g}", [P, G], U32) for g in range(2)]
+        w8_last = sb("w8_last", [P, 2, G], U32)
         up_t = sb("up_t", [P, 2 * M], U8)
         w8_view = w8_words.rearrange("a p n i -> p a (n i)")
-        w4_view = w4_words.rearrange("a p b -> p a b")
 
-        def load_k(tile, src, c, j0=0, j1=PACK):
-            rows = src[512 * c : 512 * (c + 1), :].rearrange("(p j) w -> p j w", j=PACK)
-            nc.sync.dma_start(out=tile[:], in_=rows[:, j0:j1, :])
+        def load_k(tile, src, c, cols=slice(0, T)):
+            rows = src[512 * c : 512 * (c + 1), cols].rearrange("(p j) w -> p j w", j=PACK)
+            nc.sync.dma_start(out=tile[:], in_=rows)
 
         def load_bytes(tile, src):
             nc.sync.dma_start(out=tile[:].bitcast(I32), in_=src.bitcast(I32))
 
-        load_bytes(w4_early, w4_view[:, :, : 2 * EARLY])
+        load_bytes(w4_t, w4_words.rearrange("a p b -> p a b"))
         load_w4_scales()
-        load_bytes(w8_early[0], w8_view[:, 0, : 4 * EARLY])
         load_k(x_raw[2], x, 2)
         load_k(x_raw[3], x, 3)
         load_w8_scales()
-        load_bytes(w8_early[1], w8_view[:, 1, : 4 * EARLY])
+        load_bytes(w8_first, w8_view[:, 0, : 8 * G])
         load_k(x_raw[0], x, 0)
-        load_k(x_raw[1], x, 1)
-        for c in range(3):
+        for c in (1, 2, 3, 0):
             load_k(d_raw[c], down, c)
-        for i in range(2):
-            load_k(d_raw_half[i], down, 3, 2 * i, 2 * i + 2)
-        load_bytes(w8_late, w8_view[:, :, 4 * EARLY :])
+        for h in range(2):
+            load_k(x_raw_half[h], x, 1, slice(T // 2 * h, T // 2 * (h + 1)))
+        load_bytes(w8_second[0], w8_view[:, 1, : 4 * G])
 
         x_q = [sb(f"x_q{c}", [P, T], U32) for c in range(4)]
         x_s = [sb(f"x_s{c}", [P, T], U8) for c in range(4)]
         x_b = [sb(f"x_b{c}", [P, PACK * T], BF16) for c in range(4)]
+        d_q = [sb(f"d_q{c}", [P, R], U32) for c in range(4)]
+        d_s = [sb(f"d_s{c}", [P, R], U8) for c in range(4)]
+        d_b = [sb(f"d_b{c}", [P, PACK * R], BF16) for c in range(4)]
+        h_q = sb("h_q", [P, T], U32)
+        h_s = sb("h_s", [P, T], U8)
+        h_b = sb("h_b", [P, PACK * T], BF16)
+        part = {i: sb(f"part{i}", [P, T], F32) for i in range(4, 12)}
 
         def interleave(copy, dst, raw, a, b):
             copy(
@@ -98,147 +103,158 @@ def tile_mix_three_fm_none_kernel(
                 raw[:, :, a:b].rearrange("p t (c i) -> p c t i", i=4),
             )
 
+        def permute(copy, dst, raw, a, b):
+            copy(
+                dst[:].rearrange("p (t m j) -> p m j t", t=4, j=4)[:, a:b],
+                raw[:].rearrange("p j (m t) -> p m j t", t=4)[:, a:b],
+            )
+
+        def quantize(codes, scales, values, a, b):
+            nc.vector.quantize_mx(
+                out=codes[:, a:b].bitcast(FP8X4), scales=scales[:, a:b], in_=values[:, PACK * a : PACK * b]
+            )
+
+        def prepare_x(c):
+            interleave(nc.vector.tensor_copy, x_b[c], x_raw[c], 0, X_VEC)
+            interleave(nc.scalar.copy, x_b[c], x_raw[c], X_VEC, T)
+            quantize(x_q[c], x_s[c], x_b[c], 0, T)
+
+        def prepare_x_half(h):
+            dst = x_b[1][:, PACK * T // 2 * h : PACK * T // 2 * (h + 1)]
+            interleave(nc.vector.tensor_copy, dst, x_raw_half[h], 0, HALF_VEC)
+            interleave(nc.scalar.copy, dst, x_raw_half[h], HALF_VEC, T // 2)
+            for q in (2 * h, 2 * h + 1):
+                quantize(x_q[1], x_s[1], x_b[1], P * q, P * (q + 1))
+
+        def prepare_down(c):
+            permute(nc.vector.tensor_copy, d_b[c], d_raw[c], 0, D_VEC)
+            permute(nc.scalar.copy, d_b[c], d_raw[c], D_VEC, P)
+            quantize(d_q[c], d_s[c], d_b[c], 0, R)
+
         def bank(b, shape):
             return psum.tile(shape, F32, name=f"bank{b}")
 
         acc = {}
+        h_acc = {}
 
-        def w_pass(i, c, start, stop):
-            early = P * i < EARLY
-            n = i if early else i - EARLY // P
-            if c < 2:
-                words = w8_early[c][:] if early else w8_late[:, c, :]
-                lhs = words[:, P * n : P * (n + 1)].bitcast(FP8X4)
-                lhs_scale = w8_plane[W8_ROW:P, c, P * i : P * (i + 1)]
-            else:
-                words = w4_early if early else w4_late
-                lhs = words[:, c - 2, 2 * P * n : 2 * P * (n + 1)].bitcast(FP4X4)
+        def w_pass(i, c, start=False, stop=False):
+            g, n = divmod(i, 4)
+            if c >= 2:
+                lhs = w4_t[:, c - 2, 2 * P * i : 2 * P * (i + 1)].bitcast(FP4X4)
                 lhs_scale = w4_plane[:, c - 2, P * i : P * (i + 1)]
+            else:
+                if g == 2:
+                    words = w8_last[:, c, P * n : P * (n + 1)]
+                elif c == 0:
+                    words = w8_first[:, P * i : P * (i + 1)]
+                else:
+                    words = w8_second[g][:, P * n : P * (n + 1)]
+                lhs = words.bitcast(FP8X4)
+                lhs_scale = w8_plane[W8_ROW:P, c, P * i : P * (i + 1)]
             nc.tensor.matmul_mx(
                 out=acc[i][:], lhsT=lhs, lhsT_scale=lhs_scale,
                 rhs=x_q[c][:].bitcast(FP8X4), rhs_scale=x_s[c][:], start=start, stop=stop,
             )
 
-        for i in range(8):
-            acc[i] = bank(i, [P, T])
-        for c in (2, 3, 0, 1):
-            interleave(nc.vector.tensor_copy, x_b[c], x_raw[c], 0, X_VEC)
-            interleave(nc.scalar.copy, x_b[c], x_raw[c], X_VEC, T)
-            nc.vector.quantize_mx(out=x_q[c][:].bitcast(FP8X4), scales=x_s[c][:], in_=x_b[c][:])
-            for i in range(8):
-                w_pass(i, c, c == 2, c == 1 and i < 4)
+        def park(i, copy):
+            copy(part[i][:], acc[i][:])
+
+        def h_passes(q, c):
+            cols = slice(P * q, P * (q + 1))
+            for t in range(4):
+                rows = slice(P * t, P * (t + 1))
+                nc.tensor.matmul_mx(
+                    out=h_acc[q][:, t, :], lhsT=d_q[c][:, rows].bitcast(FP8X4), lhsT_scale=d_s[c][:, rows],
+                    rhs=x_q[c][:, cols].bitcast(FP8X4), rhs_scale=x_s[c][:, cols],
+                    start=(c == 2 and t == 0), stop=(c == 1 and t == 3),
+                )
+
+        def h_out(copy, q):
+            copy(
+                h_b[:, PACK * P * q : PACK * P * (q + 1)].rearrange("p (n t) -> p n t", t=4),
+                h_acc[q][:].rearrange("p t n -> p n t"),
+            )
+
+        def finish(i, copy=None):
+            nc.tensor.matmul_mx(
+                out=acc[i][:], lhsT=up_t[:, 2 * P * i : 2 * P * (i + 1)].bitcast(FP4X4),
+                lhsT_scale=up_plane[:, P * i : P * (i + 1)],
+                rhs=h_q[:].bitcast(FP8X4), rhs_scale=h_s[:], start=False, stop=True,
+            )
+            res = sb(f"res{i}", [P, T], F32)
+            if i in part:
+                nc.vector.tensor_add(res[:], acc[i][:], part[i][:])
+            else:
+                copy(res[:], acc[i][:])
+            nc.sync.dma_start(out=out[P * i : P * (i + 1), :], in_=res[:])
+
+        on_vector = nc.vector.tensor_copy
+        on_scalar = nc.scalar.copy
+
+        for n in range(4):
+            acc[8 + n] = bank(n, [P, T])
+            acc[n] = bank(4 + n, [P, T])
+        for c in (2, 3):
+            prepare_x(c)
+            for i in (8, 9, 10, 11, 0, 1, 2, 3):
+                w_pass(i, c, start=(c == 2), stop=(c == 3 and i >= 8))
 
         nc.vector.memset(up_plane[:].bitcast(I32), 0)
         for r in range(4):
             nc.sync.dma_start(out=up_plane[r:P:32, :].bitcast(I32), in_=up_rows[r][:, 0, :].bitcast(I32))
         load_bytes(up_t, up_words[0])
-        load_bytes(w4_late, w4_view[:, :, 2 * EARLY :])
+        load_bytes(w8_second[1], w8_view[:, 1, 4 * G : 8 * G])
+        load_bytes(w8_last, w8_view[:, :, 8 * G :])
 
-        part = [sb(f"part{i}", [P, T], F32) for i in range(4)]
-
-        d_q = [sb(f"d_q{c}", [P, R], U32) for c in range(4)]
-        d_s = [sb(f"d_s{c}", [P, R], U8) for c in range(4)]
-        d_b = [sb(f"d_b{c}", [P, PACK * R], BF16) for c in range(4)]
-        h_acc = []
-
-        def permute(copy, dst, raw, a, b, j0=0, j1=PACK):
-            copy(
-                dst[:].rearrange("p (t m j) -> p m j t", t=4, j=4)[:, a:b, j0:j1],
-                raw[:].rearrange("p j (m t) -> p m j t", t=4)[:, a:b],
-            )
-
-        def h_pass(t, q, c):
-            rows = slice(P * t, P * (t + 1))
-            cols = slice(P * q, P * (q + 1))
-            nc.tensor.matmul_mx(
-                out=h_acc[q][:, t, :], lhsT=d_q[c][:, rows].bitcast(FP8X4), lhsT_scale=d_s[c][:, rows],
-                rhs=x_q[c][:, cols].bitcast(FP8X4), rhs_scale=x_s[c][:, cols],
-                start=(c == 0 and t == 0), stop=(c == 3 and t == 3),
-            )
-
-        for c in range(3):
-            permute(nc.vector.tensor_copy, d_b[c], d_raw[c], 0, D_VEC)
-            permute(nc.scalar.copy, d_b[c], d_raw[c], D_VEC, P)
-            nc.vector.quantize_mx(out=d_q[c][:].bitcast(FP8X4), scales=d_s[c][:], in_=d_b[c][:])
-            if c == 0:
-                for i in range(4):
-                    copy = nc.vector.tensor_copy if i == 3 else nc.scalar.copy
-                    copy(part[i][:], acc[i][:])
-                    h_acc.append(bank(i, [P, PACK, P]))
-            for t in range(4):
-                for q in range(4):
-                    h_pass(t, q, c)
-        for i in range(2):
-            permute(nc.vector.tensor_copy, d_b[3], d_raw_half[i], 0, D_VEC, 2 * i, 2 * i + 2)
-            permute(nc.scalar.copy, d_b[3], d_raw_half[i], D_VEC, P, 2 * i, 2 * i + 2)
-        for t in range(4):
-            rows = slice(P * t, P * (t + 1))
-            nc.vector.quantize_mx(
-                out=d_q[3][:, rows].bitcast(FP8X4), scales=d_s[3][:, rows],
-                in_=d_b[3][:, 512 * t : 512 * (t + 1)],
-            )
-            h_pass(t, 0, 3)
-            h_pass(t, 1, 3)
-        for q in (2, 3):
-            for t in range(4):
-                h_pass(t, q, 3)
-
-        h_b = sb("h_b", [P, PACK * T], BF16)
-        h_q = sb("h_q", [P, T], U32)
-        h_s = sb("h_s", [P, T], U8)
-
-        def h_out(copy, q):
-            copy(
-                h_b[:, 512 * q : 512 * (q + 1)].rearrange("p (n t) -> p n t", t=4),
-                h_acc[q][:].rearrange("p t n -> p n t"),
-            )
-
-        def h_quantize(q0, q1):
-            cols = slice(P * q0, P * q1)
-            nc.vector.quantize_mx(
-                out=h_q[:, cols].bitcast(FP8X4), scales=h_s[:, cols], in_=h_b[:, 512 * q0 : 512 * q1]
-            )
-
-        h_out(nc.scalar.copy, 0)
-        h_out(nc.vector.tensor_copy, 1)
-        h_out(nc.scalar.copy, 2)
-        h_quantize(0, 1)
-        h_out(nc.vector.tensor_copy, 3)
-        h_quantize(1, 3)
-        h_quantize(3, 4)
-
-        def w_late(i, passes):
-            if 0 in passes:
-                acc[i] = bank(i - 8, [P, T])
-            for c in passes:
-                w_pass(i, c, c == 0, False)
-
-        def finish(i, on_scalar=False):
-            if i < 4:
-                acc[i] = bank(4 + i, [P, T])
-            nc.tensor.matmul_mx(
-                out=acc[i][:], lhsT=up_t[:, 2 * P * i : 2 * P * (i + 1)].bitcast(FP4X4),
-                lhsT_scale=up_plane[:, P * i : P * (i + 1)],
-                rhs=h_q[:].bitcast(FP8X4), rhs_scale=h_s[:], start=(i < 4), stop=True,
-            )
-            res = sb(f"res{i}", [P, T], F32)
-            if i < 4:
-                nc.vector.tensor_add(res[:], acc[i][:], part[i][:])
-            elif on_scalar:
-                nc.scalar.copy(res[:], acc[i][:])
-            else:
-                nc.vector.tensor_copy(res[:], acc[i][:])
-            nc.sync.dma_start(out=out[P * i : P * (i + 1), :], in_=res[:])
-
-        w_late(8, (0, 1))
-        w_late(9, (0, 1))
+        prepare_x(0)
+        park(8, on_scalar)
+        park(9, on_scalar)
+        park(10, on_vector)
+        prepare_down(1)
+        park(11, on_scalar)
         for i in range(4, 8):
-            finish(i, i % 2 == 0)
-        for i in (8, 9):
-            w_late(i, (2, 3))
-            finish(i, True)
-            finish(2 * (i - 8))
-            finish(2 * (i - 8) + 1)
-        for i in (10, 11):
-            w_late(i, (0, 1, 2, 3))
-            finish(i, True)
+            acc[i] = bank(i - 4, [P, T])
+            for c in (2, 3, 0):
+                w_pass(i, c, start=(c == 2), stop=(c == 0))
+        for i in range(4):
+            w_pass(i, 0)
+        park(4, on_scalar)
+        prepare_down(2)
+        park(5, on_scalar)
+        park(6, on_scalar)
+        park(7, on_vector)
+        for q in range(4):
+            h_acc[q] = bank(q, [P, PACK, P])
+        for c in (2, 3, 0):
+            if c != 2:
+                prepare_down(c)
+            for q in range(4):
+                h_passes(q, c)
+
+        prepare_x_half(0)
+        h_passes(0, 1)
+        h_passes(1, 1)
+        prepare_x_half(1)
+        h_passes(2, 1)
+        h_passes(3, 1)
+        h_out(on_scalar, 0)
+        h_out(on_scalar, 1)
+        quantize(h_q, h_s, h_b, 0, P)
+        h_out(on_vector, 2)
+        h_out(on_scalar, 3)
+        for q in range(1, 4):
+            quantize(h_q, h_s, h_b, P * q, P * (q + 1))
+
+        for i in range(4):
+            w_pass(i, 1)
+        for i in range(4):
+            finish(i, on_vector if i == 1 else on_scalar)
+        for i in range(4, 8):
+            acc[i] = bank(i - 4, [P, T])
+            w_pass(i, 1, start=True)
+            finish(i)
+        for i in range(8, 12):
+            acc[i] = bank(i - 4, [P, T])
+            w_pass(i, 0, start=True)
+            w_pass(i, 1)
+            finish(i)

@@ -15,11 +15,11 @@ FP4X4 = mybir.dt.float4_e2m1fn_x4
 
 P = 128
 PACK = 4
-G = 512
+EARLY = 7
 W8_ROW = 4
 X_VEC = 320
 D_VEC = 84
-HALF_VEC = 164
+HALF_VEC = 128
 
 
 def tile_mix_three_fm_none_kernel(
@@ -60,9 +60,7 @@ def tile_mix_three_fm_none_kernel(
         x_raw_half = [sb(f"x_raw1_{h}", [P, PACK, T // 2], F32) for h in range(2)]
         d_raw = [sb(f"d_raw{c}", [P, PACK, R], F32) for c in range(4)]
         w4_t = sb("w4_t", [P, 2, 2 * M], U8)
-        w8_first = sb("w8_first", [P, 2 * G], U32)
-        w8_second = [sb(f"w8_second{g}", [P, G], U32) for g in range(2)]
-        w8_last = sb("w8_last", [P, 2, G], U32)
+        w8_t = {}
         up_t = sb("up_t", [P, 2 * M], U8)
         w8_view = w8_words.rearrange("a p n i -> p a (n i)")
 
@@ -73,18 +71,24 @@ def tile_mix_three_fm_none_kernel(
         def load_bytes(tile, src):
             nc.sync.dma_start(out=tile[:].bitcast(I32), in_=src.bitcast(I32))
 
+        def load_w8(a, first, last):
+            tile = sb(f"w8_{a}_{first}", [P, P * (last - first)], U32)
+            load_bytes(tile, w8_view[:, a, 4 * P * first : 4 * P * last])
+            for i in range(first, last):
+                w8_t[a, i] = tile[:, P * (i - first) : P * (i - first + 1)]
+
         load_bytes(w4_t, w4_words.rearrange("a p b -> p a b"))
         load_w4_scales()
         load_k(x_raw[2], x, 2)
         load_k(x_raw[3], x, 3)
         load_w8_scales()
-        load_bytes(w8_first, w8_view[:, 0, : 8 * G])
+        load_w8(0, 0, EARLY)
         load_k(x_raw[0], x, 0)
         for c in (1, 2, 3, 0):
             load_k(d_raw[c], down, c)
         for h in range(2):
             load_k(x_raw_half[h], x, 1, slice(T // 2 * h, T // 2 * (h + 1)))
-        load_bytes(w8_second[0], w8_view[:, 1, : 4 * G])
+        load_w8(1, 0, 4)
 
         x_q = [sb(f"x_q{c}", [P, T], U32) for c in range(4)]
         x_s = [sb(f"x_s{c}", [P, T], U8) for c in range(4)]
@@ -137,23 +141,16 @@ def tile_mix_three_fm_none_kernel(
         acc = {}
         h_acc = {}
 
-        def w_pass(i, c, start=False, stop=False):
-            g, n = divmod(i, 4)
+        def w_pass(i, c, start=False, stop=False, cols=slice(0, T), dst=None):
             if c >= 2:
                 lhs = w4_t[:, c - 2, 2 * P * i : 2 * P * (i + 1)].bitcast(FP4X4)
                 lhs_scale = w4_plane[:, c - 2, P * i : P * (i + 1)]
             else:
-                if g == 2:
-                    words = w8_last[:, c, P * n : P * (n + 1)]
-                elif c == 0:
-                    words = w8_first[:, P * i : P * (i + 1)]
-                else:
-                    words = w8_second[g][:, P * n : P * (n + 1)]
-                lhs = words.bitcast(FP8X4)
+                lhs = w8_t[c, i].bitcast(FP8X4)
                 lhs_scale = w8_plane[W8_ROW:P, c, P * i : P * (i + 1)]
             nc.tensor.matmul_mx(
-                out=acc[i][:], lhsT=lhs, lhsT_scale=lhs_scale,
-                rhs=x_q[c][:].bitcast(FP8X4), rhs_scale=x_s[c][:], start=start, stop=stop,
+                out=acc[i][:] if dst is None else dst, lhsT=lhs, lhsT_scale=lhs_scale,
+                rhs=x_q[c][:, cols].bitcast(FP8X4), rhs_scale=x_s[c][:, cols], start=start, stop=stop,
             )
 
         def park(i, copy):
@@ -175,18 +172,24 @@ def tile_mix_three_fm_none_kernel(
                 h_acc[q][:].rearrange("p t n -> p n t"),
             )
 
-        def finish(i, copy=None):
+        def up_pass(i, dst, cols=slice(0, T), stop=True):
             nc.tensor.matmul_mx(
-                out=acc[i][:], lhsT=up_t[:, 2 * P * i : 2 * P * (i + 1)].bitcast(FP4X4),
+                out=dst, lhsT=up_t[:, 2 * P * i : 2 * P * (i + 1)].bitcast(FP4X4),
                 lhsT_scale=up_plane[:, P * i : P * (i + 1)],
-                rhs=h_q[:].bitcast(FP8X4), rhs_scale=h_s[:], start=False, stop=True,
+                rhs=h_q[:, cols].bitcast(FP8X4), rhs_scale=h_s[:, cols], start=False, stop=stop,
             )
-            res = sb(f"res{i}", [P, T], F32)
+
+        def store(i, sums, copy=None, cols=slice(0, T)):
+            res = sb(f"res{i}_{cols.start}", [P, cols.stop - cols.start], F32)
             if i in part:
-                nc.vector.tensor_add(res[:], acc[i][:], part[i][:])
+                nc.vector.tensor_add(res[:], sums, part[i][:, cols])
             else:
-                copy(res[:], acc[i][:])
-            nc.sync.dma_start(out=out[P * i : P * (i + 1), :], in_=res[:])
+                copy(res[:], sums)
+            nc.sync.dma_start(out=out[P * i : P * (i + 1), cols], in_=res[:])
+
+        def finish(i, copy=None):
+            up_pass(i, acc[i][:])
+            store(i, acc[i][:], copy)
 
         on_vector = nc.vector.tensor_copy
         on_scalar = nc.scalar.copy
@@ -203,8 +206,9 @@ def tile_mix_three_fm_none_kernel(
         for r in range(4):
             nc.sync.dma_start(out=up_plane[r:P:32, :].bitcast(I32), in_=up_rows[r][:, 0, :].bitcast(I32))
         load_bytes(up_t, up_words[0])
-        load_bytes(w8_second[1], w8_view[:, 1, 4 * G : 8 * G])
-        load_bytes(w8_last, w8_view[:, :, 8 * G :])
+        load_w8(1, 4, 8)
+        load_w8(0, EARLY, 12)
+        load_w8(1, 8, 12)
 
         prepare_x(0)
         park(8, on_scalar)
@@ -214,8 +218,9 @@ def tile_mix_three_fm_none_kernel(
         park(11, on_scalar)
         for i in range(4, 8):
             acc[i] = bank(i - 4, [P, T])
-            for c in (2, 3, 0):
-                w_pass(i, c, start=(c == 2), stop=(c == 0))
+            passes = (2, 3, 0) if i < EARLY else (2, 3)
+            for c in passes:
+                w_pass(i, c, start=(c == 2), stop=(c == passes[-1]))
         for i in range(4):
             w_pass(i, 0)
         park(4, on_scalar)
@@ -247,14 +252,17 @@ def tile_mix_three_fm_none_kernel(
 
         for i in range(4):
             w_pass(i, 1)
-        for i in range(4):
+        for q in range(4):
+            cols = slice(P * q, P * (q + 1))
+            up_pass(0, acc[0][:, cols], cols, stop=(q == 3))
+        for h in range(2):
+            cols = slice(T // 2 * h, T // 2 * (h + 1))
+            store(0, acc[0][:, cols], on_scalar, cols)
+        for i in range(1, 4):
             finish(i, on_vector if i == 1 else on_scalar)
-        for i in range(4, 8):
+        for i in range(4, 12):
             acc[i] = bank(i - 4, [P, T])
-            w_pass(i, 1, start=True)
-            finish(i)
-        for i in range(8, 12):
-            acc[i] = bank(i - 4, [P, T])
-            w_pass(i, 0, start=True)
-            w_pass(i, 1)
+            if i >= EARLY:
+                w_pass(i, 0, start=True)
+            w_pass(i, 1, start=(i < EARLY))
             finish(i)

@@ -15,9 +15,10 @@ FP4X4 = mybir.dt.float4_e2m1fn_x4
 
 P = 128
 PACK = 4
-EARLY = 7
+EARLY = 8
 W8_ROW = 4
 X_VEC = 320
+X_VEC_LOW = 96
 D_VEC = 84
 HALF_VEC = 128
 
@@ -118,10 +119,9 @@ def tile_mix_three_fm_none_kernel(
                 out=codes[:, a:b].bitcast(FP8X4), scales=scales[:, a:b], in_=values[:, PACK * a : PACK * b]
             )
 
-        def prepare_x(c):
-            interleave(nc.vector.tensor_copy, x_b[c], x_raw[c], 0, X_VEC)
-            interleave(nc.scalar.copy, x_b[c], x_raw[c], X_VEC, T)
-            quantize(x_q[c], x_s[c], x_b[c], 0, T)
+        def round_x(c, share):
+            interleave(nc.vector.tensor_copy, x_b[c], x_raw[c], 0, share)
+            interleave(nc.scalar.copy, x_b[c], x_raw[c], share, T)
 
         def prepare_x_half(h):
             dst = x_b[1][:, PACK * T // 2 * h : PACK * T // 2 * (h + 1)]
@@ -198,9 +198,18 @@ def tile_mix_three_fm_none_kernel(
             acc[8 + n] = bank(n, [P, T])
             acc[n] = bank(4 + n, [P, T])
         for c in (2, 3):
-            prepare_x(c)
+            round_x(c, X_VEC if c == 2 else X_VEC_LOW)
+            quantize(x_q[c], x_s[c], x_b[c], 0, T)
             for i in (8, 9, 10, 11, 0, 1, 2, 3):
                 w_pass(i, c, start=(c == 2), stop=(c == 3 and i >= 8))
+
+        round_x(0, X_VEC_LOW)
+        park(8, on_vector)
+        park(9, on_vector)
+        park(10, on_vector)
+        park(11, on_scalar)
+        quantize(x_q[0], x_s[0], x_b[0], 0, T)
+        prepare_down(1)
 
         nc.vector.memset(up_plane[:].bitcast(I32), 0)
         for r in range(4):
@@ -210,29 +219,26 @@ def tile_mix_three_fm_none_kernel(
         load_w8(0, EARLY, 12)
         load_w8(1, 8, 12)
 
-        prepare_x(0)
-        park(8, on_scalar)
-        park(9, on_scalar)
-        park(10, on_vector)
-        prepare_down(1)
-        park(11, on_scalar)
         for i in range(4, 8):
             acc[i] = bank(i - 4, [P, T])
-            passes = (2, 3, 0) if i < EARLY else (2, 3)
-            for c in passes:
-                w_pass(i, c, start=(c == 2), stop=(c == passes[-1]))
-        for i in range(4):
-            w_pass(i, 0)
-        park(4, on_scalar)
+            w_pass(i, 2, start=True)
+            w_pass(i, 3)
+        for i in range(4, 8):
+            w_pass(i, 0, stop=True)
+        w_pass(0, 0)
+        w_pass(1, 0)
         prepare_down(2)
+        park(4, on_scalar)
         park(5, on_scalar)
-        park(6, on_scalar)
-        park(7, on_vector)
+        park(6, on_vector)
+        park(7, on_scalar)
         for q in range(4):
             h_acc[q] = bank(q, [P, PACK, P])
-        for c in (2, 3, 0):
-            if c != 2:
-                prepare_down(c)
+            h_passes(q, 2)
+        w_pass(2, 0)
+        w_pass(3, 0)
+        for c in (3, 0):
+            prepare_down(c)
             for q in range(4):
                 h_passes(q, c)
 
@@ -260,9 +266,18 @@ def tile_mix_three_fm_none_kernel(
             store(0, acc[0][:, cols], on_scalar, cols)
         for i in range(1, 4):
             finish(i, on_vector if i == 1 else on_scalar)
-        for i in range(4, 12):
+        for i in range(4, 11):
             acc[i] = bank(i - 4, [P, T])
             if i >= EARLY:
                 w_pass(i, 0, start=True)
             w_pass(i, 1, start=(i < EARLY))
             finish(i)
+        width = T // 2
+        for s in range(2):
+            cols = slice(width * s, width * (s + 1))
+            sums = bank(s, [P, width])
+            w_pass(11, 0, start=True, cols=cols, dst=sums[:])
+            w_pass(11, 1, cols=cols, dst=sums[:])
+            for n in range(0, width, P):
+                up_pass(11, sums[:, n : n + P], slice(cols.start + n, cols.start + n + P), stop=(n + P == width))
+            store(11, sums[:], cols=cols)

@@ -19,7 +19,8 @@ EARLY = 8
 W8_ROW = 4
 X_VEC = 320
 X_VEC_LOW = 96
-D_VEC = 84
+D_VEC_HIGH = 88
+D_VEC = 80
 HALF_VEC = 128
 
 
@@ -43,6 +44,7 @@ def tile_mix_three_fm_none_kernel(
         nc.vector.memset(warm_in[:], 0.0)
         nc.vector.memset(w4_plane[:].rearrange("p a n -> p (a n)").bitcast(I32), 0)
         nc.vector.memset(w8_plane[:].rearrange("p a n -> p (a n)").bitcast(I32), 0)
+        nc.vector.memset(up_plane[:].bitcast(I32), 0)
         nc.scalar.copy(warm_out[:], warm_in[:])
 
         w8_rows = w8_scales.rearrange("a (q r) n -> r q a n", r=4)
@@ -85,11 +87,17 @@ def tile_mix_three_fm_none_kernel(
         load_w8_scales()
         load_w8(0, 0, EARLY)
         load_k(x_raw[0], x, 0)
-        for c in (1, 2, 3, 0):
+        for c in (2, 3, 0, 1):
             load_k(d_raw[c], down, c)
         for h in range(2):
             load_k(x_raw_half[h], x, 1, slice(T // 2 * h, T // 2 * (h + 1)))
         load_w8(1, 0, 4)
+        for r in range(4):
+            nc.sync.dma_start(out=up_plane[r:P:32, :].bitcast(I32), in_=up_rows[r][:, 0, :].bitcast(I32))
+        load_bytes(up_t, up_words[0])
+        load_w8(1, 4, 8)
+        load_w8(0, EARLY, 12)
+        load_w8(1, 8, 12)
 
         x_q = [sb(f"x_q{c}", [P, T], U32) for c in range(4)]
         x_s = [sb(f"x_s{c}", [P, T], U8) for c in range(4)]
@@ -130,9 +138,9 @@ def tile_mix_three_fm_none_kernel(
             for q in (2 * h, 2 * h + 1):
                 quantize(x_q[1], x_s[1], x_b[1], P * q, P * (q + 1))
 
-        def prepare_down(c):
-            permute(nc.vector.tensor_copy, d_b[c], d_raw[c], 0, D_VEC)
-            permute(nc.scalar.copy, d_b[c], d_raw[c], D_VEC, P)
+        def prepare_down(c, share):
+            permute(nc.vector.tensor_copy, d_b[c], d_raw[c], 0, share)
+            permute(nc.scalar.copy, d_b[c], d_raw[c], share, P)
             quantize(d_q[c], d_s[c], d_b[c], 0, R)
 
         def bank(b, shape):
@@ -209,15 +217,7 @@ def tile_mix_three_fm_none_kernel(
         park(10, on_vector)
         park(11, on_scalar)
         quantize(x_q[0], x_s[0], x_b[0], 0, T)
-        prepare_down(1)
-
-        nc.vector.memset(up_plane[:].bitcast(I32), 0)
-        for r in range(4):
-            nc.sync.dma_start(out=up_plane[r:P:32, :].bitcast(I32), in_=up_rows[r][:, 0, :].bitcast(I32))
-        load_bytes(up_t, up_words[0])
-        load_w8(1, 4, 8)
-        load_w8(0, EARLY, 12)
-        load_w8(1, 8, 12)
+        prepare_down(2, D_VEC)
 
         for i in range(4, 8):
             acc[i] = bank(i - 4, [P, T])
@@ -225,22 +225,21 @@ def tile_mix_three_fm_none_kernel(
             w_pass(i, 3)
         for i in range(4, 8):
             w_pass(i, 0, stop=True)
-        w_pass(0, 0)
-        w_pass(1, 0)
-        prepare_down(2)
-        park(4, on_scalar)
-        park(5, on_scalar)
-        park(6, on_vector)
-        park(7, on_scalar)
+        for pair, c in enumerate((3, 0)):
+            prepare_down(c, D_VEC_HIGH)
+            for q in (2 * pair, 2 * pair + 1):
+                park(4 + q, on_scalar)
+                h_acc[q] = bank(q, [P, PACK, P])
+                h_passes(q, 2)
+                h_passes(q, 3)
+            if pair == 0:
+                w_pass(0, 0)
+                w_pass(1, 0)
         for q in range(4):
-            h_acc[q] = bank(q, [P, PACK, P])
-            h_passes(q, 2)
+            h_passes(q, 0)
         w_pass(2, 0)
         w_pass(3, 0)
-        for c in (3, 0):
-            prepare_down(c)
-            for q in range(4):
-                h_passes(q, c)
+        prepare_down(1, D_VEC)
 
         prepare_x_half(0)
         h_passes(0, 1)

@@ -15,13 +15,13 @@ FP4X4 = mybir.dt.float4_e2m1fn_x4
 
 P = 128
 PACK = 4
-EARLY = 8
+EARLY = 10
 W8_ROW = 4
 X_VEC = 320
 X_VEC_LOW = 96
-D_VEC_HIGH = 88
-D_VEC = 80
-HALF_VEC = 128
+D_VEC_HIGH = 92
+D_VEC = 76
+HALF_VEC = 160
 
 
 def tile_mix_three_fm_none_kernel(
@@ -133,7 +133,8 @@ def tile_mix_three_fm_none_kernel(
 
         def prepare_x_half(h):
             dst = x_b[1][:, PACK * T // 2 * h : PACK * T // 2 * (h + 1)]
-            interleave(nc.vector.tensor_copy, dst, x_raw_half[h], 0, HALF_VEC)
+            interleave(nc.vector.tensor_copy, dst, x_raw_half[h], 0, P)
+            interleave(nc.vector.tensor_copy, dst, x_raw_half[h], P, HALF_VEC)
             interleave(nc.scalar.copy, dst, x_raw_half[h], HALF_VEC, T // 2)
             for q in (2 * h, 2 * h + 1):
                 quantize(x_q[1], x_s[1], x_b[1], P * q, P * (q + 1))
@@ -176,8 +177,8 @@ def tile_mix_three_fm_none_kernel(
 
         def h_out(copy, q):
             copy(
-                h_b[:, PACK * P * q : PACK * P * (q + 1)].rearrange("p (n t) -> p n t", t=4),
-                h_acc[q][:].rearrange("p t n -> p n t"),
+                h_b[:, PACK * P * q : PACK * P * (q + 1)].rearrange("p (m e t) -> p m t e", e=2, t=4),
+                h_acc[q][:].rearrange("p t (m e) -> p m t e", e=2),
             )
 
         def up_pass(i, dst, cols=slice(0, T), stop=True):
@@ -208,26 +209,26 @@ def tile_mix_three_fm_none_kernel(
         for c in (2, 3):
             round_x(c, X_VEC if c == 2 else X_VEC_LOW)
             quantize(x_q[c], x_s[c], x_b[c], 0, T)
-            for i in (8, 9, 10, 11, 0, 1, 2, 3):
-                w_pass(i, c, start=(c == 2), stop=(c == 3 and i >= 8))
+            for i in (10, 11, 8, 9, 0, 1, 2, 3):
+                w_pass(i, c, start=(c == 2), stop=(c == 3 and i >= EARLY))
 
-        round_x(0, X_VEC_LOW)
-        park(8, on_vector)
-        park(9, on_vector)
-        park(10, on_vector)
+        round_x(0, X_VEC)
+        park(10, on_scalar)
         park(11, on_scalar)
         quantize(x_q[0], x_s[0], x_b[0], 0, T)
-        prepare_down(2, D_VEC)
-
-        for i in range(4, 8):
+        for i in (8, 9):
+            w_pass(i, 0, stop=True)
+        prepare_down(2, D_VEC_HIGH)
+        park(8, on_scalar)
+        park(9, on_scalar)
+        for i in (6, 7, 4, 5):
             acc[i] = bank(i - 4, [P, T])
             w_pass(i, 2, start=True)
             w_pass(i, 3)
-        for i in range(4, 8):
             w_pass(i, 0, stop=True)
         for pair, c in enumerate((3, 0)):
             prepare_down(c, D_VEC_HIGH)
-            for q in (2 * pair, 2 * pair + 1):
+            for q in (2 - 2 * pair, 3 - 2 * pair):
                 park(4 + q, on_scalar)
                 h_acc[q] = bank(q, [P, PACK, P])
                 h_passes(q, 2)

@@ -36,13 +36,14 @@ def tile_mix_three_fm_none_kernel(
         def sb(name, shape, dtype):
             return keep.tile(shape, dtype, name=name, align_bytes=256)
 
-        w4_plane = sb("w4_plane", [P, 2, M], U8)
+        w4_plane = [sb(f"w4_plane{a}", [P, M], U8) for a in range(2)]
         w8_plane = sb("w8_plane", [P, 2, M], U8)
         up_plane = sb("up_plane", [P, M], U8)
         warm_in = sb("warm_in", [P, 1], F32)
         warm_out = sb("warm_out", [P, 1], F32)
         nc.vector.memset(warm_in[:], 0.0)
-        nc.vector.memset(w4_plane[:].rearrange("p a n -> p (a n)").bitcast(I32), 0)
+        for a in range(2):
+            nc.vector.memset(w4_plane[a][:].bitcast(I32), 0)
         nc.vector.memset(w8_plane[:].rearrange("p a n -> p (a n)").bitcast(I32), 0)
         nc.vector.memset(up_plane[:].bitcast(I32), 0)
         nc.scalar.copy(warm_out[:], warm_in[:])
@@ -51,9 +52,9 @@ def tile_mix_three_fm_none_kernel(
         w4_rows = w4_scales.rearrange("a (q r) n -> r q a n", r=4)
         up_rows = up_scales.rearrange("a (q r) n -> r q a n", r=4)
 
-        def load_w4_scales():
+        def load_w4_scales(queue, a):
             for r in range(4):
-                nc.gpsimd.dma_start(out=w4_plane[r:P:32].bitcast(I32), in_=w4_rows[r].bitcast(I32))
+                queue.dma_start(out=w4_plane[a][r:P:32, :].bitcast(I32), in_=w4_rows[r][:, a, :].bitcast(I32))
 
         def load_w8_scales():
             for r in range(4):
@@ -62,7 +63,7 @@ def tile_mix_three_fm_none_kernel(
         x_raw = {c: sb(f"x_raw{c}", [P, PACK, T], F32) for c in (2, 3, 0)}
         x_raw_half = [sb(f"x_raw1_{h}", [P, PACK, T // 2], F32) for h in range(2)]
         d_raw = [sb(f"d_raw{c}", [P, PACK, R], F32) for c in range(4)]
-        w4_t = sb("w4_t", [P, 2, 2 * M], U8)
+        w4_t = [sb(f"w4_t{a}", [P, 2 * M], U8) for a in range(2)]
         w8_t = {}
         up_t = sb("up_t", [P, 2 * M], U8)
         w8_view = w8_words.rearrange("a p n i -> p a (n i)")
@@ -80,9 +81,11 @@ def tile_mix_three_fm_none_kernel(
             for i in range(first, last):
                 w8_t[a, i] = tile[:, P * (i - first) : P * (i - first + 1)]
 
-        load_bytes(w4_t, w4_words.rearrange("a p b -> p a b"))
-        load_w4_scales()
+        load_bytes(w4_t[0], w4_words[0])
+        load_w4_scales(nc.sync, 0)
+        load_w4_scales(nc.gpsimd, 1)
         load_k(x_raw[2], x, 2)
+        load_bytes(w4_t[1], w4_words[1])
         load_k(x_raw[3], x, 3)
         load_w8_scales()
         load_w8(0, 0, EARLY)
@@ -152,8 +155,8 @@ def tile_mix_three_fm_none_kernel(
 
         def w_pass(i, c, start=False, stop=False, cols=slice(0, T), dst=None):
             if c >= 2:
-                lhs = w4_t[:, c - 2, 2 * P * i : 2 * P * (i + 1)].bitcast(FP4X4)
-                lhs_scale = w4_plane[:, c - 2, P * i : P * (i + 1)]
+                lhs = w4_t[c - 2][:, 2 * P * i : 2 * P * (i + 1)].bitcast(FP4X4)
+                lhs_scale = w4_plane[c - 2][:, P * i : P * (i + 1)]
             else:
                 lhs = w8_t[c, i].bitcast(FP8X4)
                 lhs_scale = w8_plane[W8_ROW:P, c, P * i : P * (i + 1)]

@@ -17,8 +17,9 @@ P = 128
 PACK = 4
 EARLY = 10
 W8_ROW = 4
-X_VEC = 320
-X_VEC_LOW = 96
+X_VEC = 256
+X_VEC_LOW = 224
+X0_VEC = 384
 D_VEC_HIGH = 92
 D_VEC = 76
 HALF_VEC = 160
@@ -81,17 +82,18 @@ def tile_mix_three_fm_none_kernel(
             for i in range(first, last):
                 w8_t[a, i] = tile[:, P * (i - first) : P * (i - first + 1)]
 
+        load_k(x_raw[2], x, 2)
         load_bytes(w4_t[0], w4_words[0])
         load_w4_scales(nc.sync, 0)
         load_w4_scales(nc.gpsimd, 1)
-        load_k(x_raw[2], x, 2)
-        load_bytes(w4_t[1], w4_words[1])
         load_k(x_raw[3], x, 3)
+        load_bytes(w4_t[1], w4_words[1])
         load_w8_scales()
-        load_w8(0, 0, EARLY)
+        load_w8(0, 2, EARLY)
         load_k(x_raw[0], x, 0)
         for c in (2, 3, 0, 1):
             load_k(d_raw[c], down, c)
+        load_w8(0, 0, 2)
         for h in range(2):
             load_k(x_raw_half[h], x, 1, slice(T // 2 * h, T // 2 * (h + 1)))
         load_w8(1, 0, 4)
@@ -215,16 +217,20 @@ def tile_mix_three_fm_none_kernel(
             for i in (10, 11, 8, 9, 0, 1, 2, 3):
                 w_pass(i, c, start=(c == 2), stop=(c == 3 and i >= EARLY))
 
-        round_x(0, X_VEC)
         park(10, on_scalar)
         park(11, on_scalar)
+        round_x(0, X0_VEC)
         quantize(x_q[0], x_s[0], x_b[0], 0, T)
-        for i in (8, 9):
+        for i in (6, 7):
+            acc[i] = bank(i - 4, [P, T])
+            w_pass(i, 2, start=True)
+            w_pass(i, 3)
+        for i in (8, 9, 6, 7):
             w_pass(i, 0, stop=True)
         prepare_down(2, D_VEC_HIGH)
         park(8, on_scalar)
         park(9, on_scalar)
-        for i in (6, 7, 4, 5):
+        for i in (4, 5):
             acc[i] = bank(i - 4, [P, T])
             w_pass(i, 2, start=True)
             w_pass(i, 3)
@@ -237,12 +243,12 @@ def tile_mix_three_fm_none_kernel(
                 h_passes(q, 2)
                 h_passes(q, 3)
             if pair == 0:
-                w_pass(0, 0)
-                w_pass(1, 0)
+                w_pass(2, 0)
+                w_pass(3, 0)
         for q in range(4):
             h_passes(q, 0)
-        w_pass(2, 0)
-        w_pass(3, 0)
+        w_pass(0, 0)
+        w_pass(1, 0)
         prepare_down(1, D_VEC)
 
         prepare_x_half(0)

@@ -16,7 +16,7 @@ FP4X4 = mybir.dt.float4_e2m1fn_x4
 P = 128
 PACK = 4
 EARLY = 10
-W8_ROW = 4
+W8_ROW = (4, 8)
 X_VEC = 256
 X_VEC_LOW = 224
 X0_VEC = 384
@@ -38,14 +38,15 @@ def tile_mix_three_fm_none_kernel(
             return keep.tile(shape, dtype, name=name, align_bytes=256)
 
         w4_plane = [sb(f"w4_plane{a}", [P, M], U8) for a in range(2)]
-        w8_plane = sb("w8_plane", [P, 2, M], U8)
+        w8_plane = [sb(f"w8_plane{a}", [P, M], U8) for a in range(2)]
         up_plane = sb("up_plane", [P, M], U8)
         warm_in = sb("warm_in", [P, 1], F32)
         warm_out = sb("warm_out", [P, 1], F32)
         nc.vector.memset(warm_in[:], 0.0)
         for a in range(2):
             nc.vector.memset(w4_plane[a][:].bitcast(I32), 0)
-        nc.vector.memset(w8_plane[:].rearrange("p a n -> p (a n)").bitcast(I32), 0)
+        for a in range(2):
+            nc.vector.memset(w8_plane[a][:].bitcast(I32), 0)
         nc.vector.memset(up_plane[:].bitcast(I32), 0)
         nc.scalar.copy(warm_out[:], warm_in[:])
 
@@ -57,9 +58,9 @@ def tile_mix_three_fm_none_kernel(
             for r in range(4):
                 queue.dma_start(out=w4_plane[a][r:P:32, :].bitcast(I32), in_=w4_rows[r][:, a, :].bitcast(I32))
 
-        def load_w8_scales():
+        def load_w8_scales(a):
             for r in range(4):
-                nc.gpsimd.dma_start(out=w8_plane[W8_ROW + r : P : 32].bitcast(I32), in_=w8_rows[r].bitcast(I32))
+                nc.gpsimd.dma_start(out=w8_plane[a][W8_ROW[a] + r : P : 32, :].bitcast(I32), in_=w8_rows[r][:, a, :].bitcast(I32))
 
         x_raw = {c: sb(f"x_raw{c}", [P, PACK, T], F32) for c in (2, 3, 0)}
         x_raw_half = [sb(f"x_raw1_{h}", [P, PACK, T // 2], F32) for h in range(2)]
@@ -88,7 +89,8 @@ def tile_mix_three_fm_none_kernel(
         load_w4_scales(nc.gpsimd, 1)
         load_k(x_raw[3], x, 3)
         load_bytes(w4_t[1], w4_words[1])
-        load_w8_scales()
+        load_w8_scales(0)
+        load_w8_scales(1)
         load_w8(0, 2, EARLY)
         load_k(x_raw[0], x, 0)
         for c in (2, 3, 0, 1):
@@ -161,7 +163,7 @@ def tile_mix_three_fm_none_kernel(
                 lhs_scale = w4_plane[c - 2][:, P * i : P * (i + 1)]
             else:
                 lhs = w8_t[c, i].bitcast(FP8X4)
-                lhs_scale = w8_plane[W8_ROW:P, c, P * i : P * (i + 1)]
+                lhs_scale = w8_plane[c][W8_ROW[c] : P, P * i : P * (i + 1)]
             nc.tensor.matmul_mx(
                 out=acc[i][:] if dst is None else dst, lhsT=lhs, lhsT_scale=lhs_scale,
                 rhs=x_q[c][:, cols].bitcast(FP8X4), rhs_scale=x_s[c][:, cols], start=start, stop=stop,
@@ -228,27 +230,28 @@ def tile_mix_three_fm_none_kernel(
         for i in (8, 9, 6, 7):
             w_pass(i, 0, stop=True)
         prepare_down(2, D_VEC_HIGH)
-        park(8, on_scalar)
-        park(9, on_scalar)
+        for i in (8, 9, 6):
+            park(i, on_scalar)
+        w_pass(2, 0)
         for i in (4, 5):
             acc[i] = bank(i - 4, [P, T])
             w_pass(i, 2, start=True)
             w_pass(i, 3)
             w_pass(i, 0, stop=True)
-        for pair, c in enumerate((3, 0)):
-            prepare_down(c, D_VEC_HIGH)
-            for q in (2 - 2 * pair, 3 - 2 * pair):
-                park(4 + q, on_scalar)
-                h_acc[q] = bank(q, [P, PACK, P])
-                h_passes(q, 2)
-                h_passes(q, 3)
-            if pair == 0:
-                w_pass(2, 0)
-                w_pass(3, 0)
+        prepare_down(3, D_VEC_HIGH)
+        for i in (7, 4, 5):
+            park(i, on_scalar)
+        for q in range(4):
+            h_acc[q] = bank(q, [P, PACK, P])
+        for quarters in ((2, 3), (0, 1)):
+            for c in (2, 3):
+                for q in quarters:
+                    h_passes(q, c)
+        prepare_down(0, D_VEC_HIGH)
         for q in range(4):
             h_passes(q, 0)
-        w_pass(0, 0)
-        w_pass(1, 0)
+        for i in (3, 0, 1):
+            w_pass(i, 0)
         prepare_down(1, D_VEC)
 
         prepare_x_half(0)

@@ -95,9 +95,9 @@ def tile_mix_three_fm_none_kernel(
         load_k(x_raw[0], x, 0)
         for c in (2, 3, 0, 1):
             load_k(d_raw[c], down, c)
+        load_k(x_raw_half[0], x, 1, slice(0, T // 2))
         load_w8(0, 0, 2)
-        for h in range(2):
-            load_k(x_raw_half[h], x, 1, slice(T // 2 * h, T // 2 * (h + 1)))
+        load_k(x_raw_half[1], x, 1, slice(T // 2, T))
         load_w8(1, 0, 4)
         for r in range(4):
             nc.sync.dma_start(out=up_plane[r:P:32, :].bitcast(I32), in_=up_rows[r][:, 0, :].bitcast(I32))
@@ -124,10 +124,11 @@ def tile_mix_three_fm_none_kernel(
             )
 
         def permute(copy, dst, raw, a, b):
-            copy(
-                dst[:].rearrange("p (t m j) -> p m j t", t=4, j=4)[:, a:b],
-                raw[:].rearrange("p j (m t) -> p m j t", t=4)[:, a:b],
-            )
+            for u in range(2):
+                copy(
+                    dst[:].rearrange("p (u e m j) -> p u m j e", u=2, e=2, j=4)[:, u, a:b],
+                    raw[:].rearrange("p j (m u e) -> p u m j e", u=2, e=2)[:, u, a:b],
+                )
 
         def quantize(codes, scales, values, a, b):
             nc.vector.quantize_mx(

@@ -15,7 +15,7 @@ FP4X4 = mybir.dt.float4_e2m1fn_x4
 
 P = 128
 PACK = 4
-EARLY = 10
+EARLY = 8
 W8_ROW = (4, 8)
 X_VEC = 256
 X_VEC_LOW = 224
@@ -91,19 +91,18 @@ def tile_mix_three_fm_none_kernel(
         load_bytes(w4_t[1], w4_words[1])
         load_w8_scales(0)
         load_w8_scales(1)
-        load_w8(0, 2, EARLY)
+        load_w8(0, 0, EARLY)
         load_k(x_raw[0], x, 0)
         for c in (2, 3, 0, 1):
             load_k(d_raw[c], down, c)
         load_k(x_raw_half[0], x, 1, slice(0, T // 2))
-        load_w8(0, 0, 2)
         load_k(x_raw_half[1], x, 1, slice(T // 2, T))
         load_w8(1, 0, 4)
         for r in range(4):
             nc.sync.dma_start(out=up_plane[r:P:32, :].bitcast(I32), in_=up_rows[r][:, 0, :].bitcast(I32))
         load_bytes(up_t, up_words[0])
         load_w8(1, 4, 8)
-        load_w8(0, EARLY, 12)
+        load_w8(0, 8, 12)
         load_w8(1, 8, 12)
 
         x_q = [sb(f"x_q{c}", [P, T], U32) for c in range(4)]
@@ -150,7 +149,8 @@ def tile_mix_three_fm_none_kernel(
         def prepare_down(c, share):
             permute(nc.vector.tensor_copy, d_b[c], d_raw[c], 0, share)
             permute(nc.scalar.copy, d_b[c], d_raw[c], share, P)
-            quantize(d_q[c], d_s[c], d_b[c], 0, R)
+            for u in range(2):
+                quantize(d_q[c], d_s[c], d_b[c], R // 2 * u, R // 2 * (u + 1))
 
         def bank(b, shape):
             return psum.tile(shape, F32, name=f"bank{b}")
@@ -217,45 +217,39 @@ def tile_mix_three_fm_none_kernel(
         for c in (2, 3):
             round_x(c, X_VEC if c == 2 else X_VEC_LOW)
             quantize(x_q[c], x_s[c], x_b[c], 0, T)
-            for i in (10, 11, 8, 9, 0, 1, 2, 3):
-                w_pass(i, c, start=(c == 2), stop=(c == 3 and i >= EARLY))
+            for i in (8, 9, 10, 11, 0, 1, 2, 3):
+                w_pass(i, c, start=(c == 2), stop=(c == 3 and i >= 8))
 
-        park(10, on_scalar)
-        park(11, on_scalar)
-        round_x(0, X0_VEC)
+        for i in range(8, 12):
+            park(i, on_scalar if i % 2 == 0 else on_vector)
+        round_x(0, 352)
         quantize(x_q[0], x_s[0], x_b[0], 0, T)
-        for i in (6, 7):
+        for i in range(4, 8):
             acc[i] = bank(i - 4, [P, T])
             w_pass(i, 2, start=True)
-            w_pass(i, 3)
-        for i in (8, 9, 6, 7):
+            w_pass(i, 3, stop=(i >= EARLY))
+        for i in range(4, EARLY):
             w_pass(i, 0, stop=True)
-        prepare_down(2, D_VEC_HIGH)
-        for i in (8, 9, 6):
+        prepare_down(2, 100)
+        for i in range(4, min(EARLY, 8)):
             park(i, on_scalar)
-        w_pass(2, 0)
-        for i in (4, 5):
-            acc[i] = bank(i - 4, [P, T])
-            w_pass(i, 2, start=True)
-            w_pass(i, 3)
-            w_pass(i, 0, stop=True)
-        prepare_down(3, D_VEC_HIGH)
-        for i in (7, 4, 5):
-            park(i, on_scalar)
+        prepare_down(3, 108)
         for q in range(4):
             h_acc[q] = bank(q, [P, PACK, P])
-        for quarters in ((2, 3), (0, 1)):
-            for c in (2, 3):
-                for q in quarters:
-                    h_passes(q, c)
-        prepare_down(0, D_VEC_HIGH)
+        for c in (2, 3):
+            for q in range(4):
+                h_passes(q, c)
+        prepare_down(0, D_VEC)
         for q in range(4):
             h_passes(q, 0)
-        for i in (3, 0, 1):
+        for i in range(4):
             w_pass(i, 0)
         prepare_down(1, D_VEC)
 
-        prepare_x_half(0)
+        interleave(nc.scalar.copy, x_b[1], x_raw_half[0], 0, 128)
+        interleave(nc.vector.tensor_copy, x_b[1], x_raw_half[0], 128, T // 2)
+        for q in range(2):
+            quantize(x_q[1], x_s[1], x_b[1], P * q, P * (q + 1))
         h_passes(0, 1)
         h_passes(1, 1)
         prepare_x_half(1)

@@ -15,14 +15,8 @@ FP4X4 = mybir.dt.float4_e2m1fn_x4
 
 P = 128
 PACK = 4
-EARLY = 8
-W8_ROW = (4, 8)
-X_VEC = 256
-X_VEC_LOW = 224
-X0_VEC = 384
-D_VEC_HIGH = 92
-D_VEC = 76
-HALF_VEC = 160
+H = T // 2
+W8_ROW = 4
 
 
 def tile_mix_three_fm_none_kernel(
@@ -37,16 +31,14 @@ def tile_mix_three_fm_none_kernel(
         def sb(name, shape, dtype):
             return keep.tile(shape, dtype, name=name, align_bytes=256)
 
-        w4_plane = [sb(f"w4_plane{a}", [P, M], U8) for a in range(2)]
-        w8_plane = [sb(f"w8_plane{a}", [P, M], U8) for a in range(2)]
+        w4_plane = sb("w4_plane", [P, 2, M], U8)
+        w8_plane = sb("w8_plane", [P, 2, M], U8)
         up_plane = sb("up_plane", [P, M], U8)
         warm_in = sb("warm_in", [P, 1], F32)
         warm_out = sb("warm_out", [P, 1], F32)
         nc.vector.memset(warm_in[:], 0.0)
-        for a in range(2):
-            nc.vector.memset(w4_plane[a][:].bitcast(I32), 0)
-        for a in range(2):
-            nc.vector.memset(w8_plane[a][:].bitcast(I32), 0)
+        nc.vector.memset(w4_plane[:].bitcast(I32), 0)
+        nc.vector.memset(w8_plane[:].bitcast(I32), 0)
         nc.vector.memset(up_plane[:].bitcast(I32), 0)
         nc.scalar.copy(warm_out[:], warm_in[:])
 
@@ -54,56 +46,61 @@ def tile_mix_three_fm_none_kernel(
         w4_rows = w4_scales.rearrange("a (q r) n -> r q a n", r=4)
         up_rows = up_scales.rearrange("a (q r) n -> r q a n", r=4)
 
-        def load_w4_scales(queue, a):
+        def load_rows(queue, plane, rows, a):
             for r in range(4):
-                queue.dma_start(out=w4_plane[a][r:P:32, :].bitcast(I32), in_=w4_rows[r][:, a, :].bitcast(I32))
+                queue.dma_start(out=plane[r:P:32, :].bitcast(I32), in_=rows[r][:, a, :].bitcast(I32))
 
-        def load_w8_scales(a):
+        def load_w4_rows(queue):
             for r in range(4):
-                nc.gpsimd.dma_start(out=w8_plane[a][W8_ROW[a] + r : P : 32, :].bitcast(I32), in_=w8_rows[r][:, a, :].bitcast(I32))
+                queue.dma_start(out=w4_plane[r:P:32].bitcast(I32), in_=w4_rows[r].bitcast(I32))
+
+        def load_w8_rows(queue):
+            for r in range(4):
+                queue.dma_start(out=w8_plane[W8_ROW + r : P : 32].bitcast(I32), in_=w8_rows[r].bitcast(I32))
 
         x_raw = {c: sb(f"x_raw{c}", [P, PACK, T], F32) for c in (2, 3, 0)}
-        x_raw_half = [sb(f"x_raw1_{h}", [P, PACK, T // 2], F32) for h in range(2)]
+        x_raw_half = [sb(f"x_raw1_{h}", [P, PACK, H], F32) for h in range(2)]
         d_raw = [sb(f"d_raw{c}", [P, PACK, R], F32) for c in range(4)]
-        w4_t = [sb(f"w4_t{a}", [P, 2 * M], U8) for a in range(2)]
-        w8_t = {}
-        up_t = sb("up_t", [P, 2 * M], U8)
+        words = {}
         w8_view = w8_words.rearrange("a p n i -> p a (n i)")
 
         def load_k(tile, src, c, cols=slice(0, T)):
             rows = src[512 * c : 512 * (c + 1), cols].rearrange("(p j) w -> p j w", j=PACK)
             nc.sync.dma_start(out=tile[:], in_=rows)
 
-        def load_bytes(tile, src):
-            nc.sync.dma_start(out=tile[:].bitcast(I32), in_=src.bitcast(I32))
+        def load_w8_both(first, last):
+            tile = sb(f"words8_{first}", [P, 2, 4 * P * (last - first)], U8)
+            nc.sync.dma_start(out=tile[:].bitcast(I32), in_=w8_view[:, :, 4 * P * first : 4 * P * last].bitcast(I32))
+            for c in range(2):
+                for i in range(first, last):
+                    words[c, i] = tile[:, c, 4 * P * (i - first) : 4 * P * (i - first + 1)]
 
-        def load_w8(a, first, last):
-            tile = sb(f"w8_{a}_{first}", [P, P * (last - first)], U32)
-            load_bytes(tile, w8_view[:, a, 4 * P * first : 4 * P * last])
+        def load_words(c, first, last):
+            width = 4 * P if c < 2 else 2 * P
+            src = w8_view[:, c, :] if c < 2 else w4_words[c - 2] if c < 4 else up_words[0]
+            tile = sb(f"words{c}_{first}", [P, width * (last - first)], U8)
+            nc.sync.dma_start(out=tile[:].bitcast(I32), in_=src[:, width * first : width * last].bitcast(I32))
             for i in range(first, last):
-                w8_t[a, i] = tile[:, P * (i - first) : P * (i - first + 1)]
+                words[c, i] = tile[:, width * (i - first) : width * (i - first + 1)]
 
         load_k(x_raw[2], x, 2)
-        load_bytes(w4_t[0], w4_words[0])
-        load_w4_scales(nc.sync, 0)
-        load_w4_scales(nc.gpsimd, 1)
         load_k(x_raw[3], x, 3)
-        load_bytes(w4_t[1], w4_words[1])
-        load_w8_scales(0)
-        load_w8_scales(1)
-        load_w8(0, 0, EARLY)
+        load_w4_rows(nc.gpsimd)
+        load_words(2, 0, 12)
+        load_words(3, 0, 12)
+        load_w8_rows(nc.gpsimd)
+        load_words(0, 4, 8)
         load_k(x_raw[0], x, 0)
         for c in (2, 3, 0, 1):
             load_k(d_raw[c], down, c)
-        load_k(x_raw_half[0], x, 1, slice(0, T // 2))
-        load_k(x_raw_half[1], x, 1, slice(T // 2, T))
-        load_w8(1, 0, 4)
-        for r in range(4):
-            nc.sync.dma_start(out=up_plane[r:P:32, :].bitcast(I32), in_=up_rows[r][:, 0, :].bitcast(I32))
-        load_bytes(up_t, up_words[0])
-        load_w8(1, 4, 8)
-        load_w8(0, 8, 12)
-        load_w8(1, 8, 12)
+        load_words(0, 0, 4)
+        load_k(x_raw_half[0], x, 1, slice(0, H))
+        load_k(x_raw_half[1], x, 1, slice(H, T))
+        load_words(1, 0, 4)
+        load_rows(nc.sync, up_plane, up_rows, 0)
+        load_words(4, 0, 12)
+        load_words(1, 4, 8)
+        load_w8_both(8, 12)
 
         x_q = [sb(f"x_q{c}", [P, T], U32) for c in range(4)]
         x_s = [sb(f"x_s{c}", [P, T], U8) for c in range(4)]
@@ -111,14 +108,17 @@ def tile_mix_three_fm_none_kernel(
         d_q = [sb(f"d_q{c}", [P, R], U32) for c in range(4)]
         d_s = [sb(f"d_s{c}", [P, R], U8) for c in range(4)]
         d_b = [sb(f"d_b{c}", [P, PACK * R], BF16) for c in range(4)]
-        h_q = sb("h_q", [P, T], U32)
-        h_s = sb("h_s", [P, T], U8)
         h_b = sb("h_b", [P, PACK * T], BF16)
-        part = {i: sb(f"part{i}", [P, T], F32) for i in range(4, 12)}
+        x_q.append(sb("h_q", [P, T], U32))
+        x_s.append(sb("h_s", [P, T], U8))
+        x_b.append(h_b)
+        part = {}
+        on_vector = nc.vector.tensor_copy
+        on_scalar = nc.scalar.copy
 
-        def interleave(copy, dst, raw, a, b):
+        def interleave(copy, dst, raw, a, b, first=0):
             copy(
-                dst[:, PACK * a : PACK * b].rearrange("p (c i t) -> p c t i", i=4, t=4),
+                dst[:, PACK * (first + a) : PACK * (first + b)].rearrange("p (c i t) -> p c t i", i=4, t=4),
                 raw[:, :, a:b].rearrange("p t (c i) -> p c t i", i=4),
             )
 
@@ -134,44 +134,52 @@ def tile_mix_three_fm_none_kernel(
                 out=codes[:, a:b].bitcast(FP8X4), scales=scales[:, a:b], in_=values[:, PACK * a : PACK * b]
             )
 
-        def round_x(c, share):
-            interleave(nc.vector.tensor_copy, x_b[c], x_raw[c], 0, share)
-            interleave(nc.scalar.copy, x_b[c], x_raw[c], share, T)
+        def quantize_x(c, a=0, b=T):
+            quantize(x_q[c], x_s[c], x_b[c], a, b)
 
-        def prepare_x_half(h):
-            dst = x_b[1][:, PACK * T // 2 * h : PACK * T // 2 * (h + 1)]
-            interleave(nc.vector.tensor_copy, dst, x_raw_half[h], 0, P)
-            interleave(nc.vector.tensor_copy, dst, x_raw_half[h], P, HALF_VEC)
-            interleave(nc.scalar.copy, dst, x_raw_half[h], HALF_VEC, T // 2)
-            for q in (2 * h, 2 * h + 1):
-                quantize(x_q[1], x_s[1], x_b[1], P * q, P * (q + 1))
+        def round_x(c, share):
+            interleave(on_vector, x_b[c], x_raw[c], 0, share)
+            interleave(on_scalar, x_b[c], x_raw[c], share, T)
 
         def prepare_down(c, share):
-            permute(nc.vector.tensor_copy, d_b[c], d_raw[c], 0, share)
-            permute(nc.scalar.copy, d_b[c], d_raw[c], share, P)
+            permute(on_vector, d_b[c], d_raw[c], 0, share)
+            permute(on_scalar, d_b[c], d_raw[c], share, P)
             for u in range(2):
                 quantize(d_q[c], d_s[c], d_b[c], R // 2 * u, R // 2 * (u + 1))
 
         def bank(b, shape):
             return psum.tile(shape, F32, name=f"bank{b}")
 
-        acc = {}
-        h_acc = {}
-
-        def w_pass(i, c, start=False, stop=False, cols=slice(0, T), dst=None):
-            if c >= 2:
-                lhs = w4_t[c - 2][:, 2 * P * i : 2 * P * (i + 1)].bitcast(FP4X4)
-                lhs_scale = w4_plane[c - 2][:, P * i : P * (i + 1)]
+        def w_pass(dst, i, c, cols=slice(0, T), start=False, stop=False):
+            tile_cols = slice(P * i, P * (i + 1))
+            if c < 2:
+                lhs, lhs_scale = words[c, i].bitcast(FP8X4), w8_plane[W8_ROW:P, c, tile_cols]
             else:
-                lhs = w8_t[c, i].bitcast(FP8X4)
-                lhs_scale = w8_plane[c][W8_ROW[c] : P, P * i : P * (i + 1)]
+                lhs = words[c, i].bitcast(FP4X4)
+                lhs_scale = w4_plane[:, c - 2, tile_cols] if c < 4 else up_plane[:, tile_cols]
             nc.tensor.matmul_mx(
-                out=acc[i][:] if dst is None else dst, lhsT=lhs, lhsT_scale=lhs_scale,
+                out=dst, lhsT=lhs, lhsT_scale=lhs_scale,
                 rhs=x_q[c][:, cols].bitcast(FP8X4), rhs_scale=x_s[c][:, cols], start=start, stop=stop,
             )
 
-        def park(i, copy):
-            copy(part[i][:], acc[i][:])
+        def half_passes(sums, g, h, c, start=False, stop=False):
+            for e in range(2):
+                w_pass(sums[:, e, :], 2 * g + e, c, slice(H * h, H * (h + 1)), start and e == 0, stop and e == 1)
+
+        def park(key, sums, copy):
+            part[key] = sb(f"part{key[0]}_{key[1]}", [P, 2, H], F32)
+            copy(part[key][:], sums[:])
+
+        def park_tile(i, sums, copy):
+            g = i // 2
+            if (g, 0) not in part:
+                both = sb(f"part{g}", [P, 2, T], F32)
+                for h in range(2):
+                    part[g, h] = both[:, :, H * h : H * (h + 1)]
+                part[g] = both
+            copy(part[g][:, i % 2, :], sums[:])
+
+        h_acc = {}
 
         def h_passes(q, c):
             cols = slice(P * q, P * (q + 1))
@@ -189,102 +197,116 @@ def tile_mix_three_fm_none_kernel(
                 h_acc[q][:].rearrange("p t (m e) -> p m t e", e=2),
             )
 
-        def up_pass(i, dst, cols=slice(0, T), stop=True):
-            nc.tensor.matmul_mx(
-                out=dst, lhsT=up_t[:, 2 * P * i : 2 * P * (i + 1)].bitcast(FP4X4),
-                lhsT_scale=up_plane[:, P * i : P * (i + 1)],
-                rhs=h_q[:, cols].bitcast(FP8X4), rhs_scale=h_s[:, cols], start=False, stop=stop,
-            )
+        out_pairs = out.rearrange("(g e p) t -> g p e t", e=2, p=P)
 
-        def store(i, sums, copy=None, cols=slice(0, T)):
-            res = sb(f"res{i}_{cols.start}", [P, cols.stop - cols.start], F32)
-            if i in part:
-                nc.vector.tensor_add(res[:], sums, part[i][:, cols])
+        def store_half_pair(g, h, sums, copy=None):
+            cols = slice(H * h, H * (h + 1))
+            res = sb(f"res_pair{g}_{h}", [P, 2, H], F32)
+            if (g, h) in part:
+                nc.vector.tensor_add(res[:], sums[:], part[g, h][:])
             else:
-                copy(res[:], sums)
+                copy(res[:], sums[:])
+            nc.sync.dma_start(out=out_pairs[g][:, :, cols], in_=res[:])
+
+        def drain(res, i, sums, copy=None, cols=slice(0, T)):
+            if i // 2 in part:
+                nc.vector.tensor_add(res, sums, part[i // 2][:, i % 2, cols])
+            else:
+                copy(res, sums)
+
+        def store_tile(i, sums, copy=None, cols=slice(0, T)):
+            res = sb(f"res{i}_{cols.start}", [P, cols.stop - cols.start], F32)
+            drain(res[:], i, sums, copy, cols)
             nc.sync.dma_start(out=out[P * i : P * (i + 1), cols], in_=res[:])
 
-        def finish(i, copy=None):
-            up_pass(i, acc[i][:])
-            store(i, acc[i][:], copy)
+        def store_group(first, res):
+            rows = out[P * first : P * (first + res.shape[1]), :].rearrange("(e p) t -> p e t", p=P)
+            nc.sync.dma_start(out=rows, in_=res[:])
 
-        on_vector = nc.vector.tensor_copy
-        on_scalar = nc.scalar.copy
-
+        acc = {}
         for n in range(4):
             acc[8 + n] = bank(n, [P, T])
             acc[n] = bank(4 + n, [P, T])
         for c in (2, 3):
-            round_x(c, X_VEC if c == 2 else X_VEC_LOW)
-            quantize(x_q[c], x_s[c], x_b[c], 0, T)
+            round_x(c, 320)
+            quantize_x(c)
+        for c in (2, 3):
             for i in (8, 9, 10, 11, 0, 1, 2, 3):
-                w_pass(i, c, start=(c == 2), stop=(c == 3 and i >= 8))
-
+                w_pass(acc[i][:], i, c, start=(c == 2), stop=(c == 3 and i >= 8))
         for i in range(8, 12):
-            park(i, on_scalar if i % 2 == 0 else on_vector)
-        round_x(0, 352)
-        quantize(x_q[0], x_s[0], x_b[0], 0, T)
+            park_tile(i, acc[i], on_scalar if i % 2 == 0 else on_vector)
+        round_x(0, 320)
+        quantize_x(0)
         for i in range(4, 8):
             acc[i] = bank(i - 4, [P, T])
-            w_pass(i, 2, start=True)
-            w_pass(i, 3, stop=(i >= EARLY))
-        for i in range(4, EARLY):
-            w_pass(i, 0, stop=True)
+            w_pass(acc[i][:], i, 2, start=True)
+            w_pass(acc[i][:], i, 3)
+        for i in range(4, 8):
+            w_pass(acc[i][:], i, 0, stop=True)
         prepare_down(2, 100)
-        for i in range(4, min(EARLY, 8)):
-            park(i, on_scalar)
-        prepare_down(3, 108)
+        for i in range(4, 8):
+            park_tile(i, acc[i], on_scalar)
+        prepare_down(3, 100)
         for q in range(4):
             h_acc[q] = bank(q, [P, PACK, P])
         for c in (2, 3):
             for q in range(4):
                 h_passes(q, c)
-        prepare_down(0, D_VEC)
+        prepare_down(0, 76)
         for q in range(4):
             h_passes(q, 0)
         for i in range(4):
-            w_pass(i, 0)
-        prepare_down(1, D_VEC)
+            w_pass(acc[i][:], i, 0)
+        prepare_down(1, 76)
 
-        interleave(nc.scalar.copy, x_b[1], x_raw_half[0], 0, 128)
-        interleave(nc.vector.tensor_copy, x_b[1], x_raw_half[0], 128, T // 2)
+        interleave(on_vector, x_b[1], x_raw_half[0], 0, P)
+        interleave(on_vector, x_b[1], x_raw_half[0], P, P + 32)
+        interleave(on_scalar, x_b[1], x_raw_half[0], P + 32, H)
         for q in range(2):
-            quantize(x_q[1], x_s[1], x_b[1], P * q, P * (q + 1))
-        h_passes(0, 1)
-        h_passes(1, 1)
-        prepare_x_half(1)
-        h_passes(2, 1)
-        h_passes(3, 1)
+            quantize_x(1, P * q, P * (q + 1))
+            h_passes(q, 1)
+        interleave(on_vector, x_b[1], x_raw_half[1], 0, 88, H)
+        interleave(on_scalar, x_b[1], x_raw_half[1], 88, P, H)
+        interleave(on_vector, x_b[1], x_raw_half[1], P, P + 80, H)
+        interleave(on_scalar, x_b[1], x_raw_half[1], P + 80, H, H)
+        for q in (2, 3):
+            quantize_x(1, P * q, P * (q + 1))
+            h_passes(q, 1)
         h_out(on_scalar, 0)
         h_out(on_scalar, 1)
-        quantize(h_q, h_s, h_b, 0, P)
+        quantize_x(4, 0, P)
         h_out(on_vector, 2)
         h_out(on_scalar, 3)
         for q in range(1, 4):
-            quantize(h_q, h_s, h_b, P * q, P * (q + 1))
+            quantize_x(4, P * q, P * (q + 1))
 
         for i in range(4):
-            w_pass(i, 1)
+            w_pass(acc[i][:], i, 1)
         for q in range(4):
             cols = slice(P * q, P * (q + 1))
-            up_pass(0, acc[0][:, cols], cols, stop=(q == 3))
+            w_pass(acc[0][:, cols], 0, 4, cols, stop=(q == 3))
         for h in range(2):
-            cols = slice(T // 2 * h, T // 2 * (h + 1))
-            store(0, acc[0][:, cols], on_scalar, cols)
-        for i in range(1, 4):
-            finish(i, on_vector if i == 1 else on_scalar)
-        for i in range(4, 11):
+            cols = slice(H * h, H * (h + 1))
+            store_tile(0, acc[0][:, cols], on_scalar, cols)
+        w_pass(acc[1][:], 1, 4, stop=True)
+        store_tile(1, acc[1][:], on_vector)
+        for first in (2, 4, 6):
+            res = sb(f"res{first}", [P, 2, T], F32)
+            for i in (first, first + 1):
+                if i >= 4:
+                    acc[i] = bank(i - 4, [P, T])
+                    w_pass(acc[i][:], i, 1, start=True)
+                w_pass(acc[i][:], i, 4, stop=True)
+                drain(res[:, i - first, :], i, acc[i][:], on_scalar)
+            store_group(first, res)
+        for i in range(8, 11):
             acc[i] = bank(i - 4, [P, T])
-            if i >= EARLY:
-                w_pass(i, 0, start=True)
-            w_pass(i, 1, start=(i < EARLY))
-            finish(i)
-        width = T // 2
-        for s in range(2):
-            cols = slice(width * s, width * (s + 1))
-            sums = bank(s, [P, width])
-            w_pass(11, 0, start=True, cols=cols, dst=sums[:])
-            w_pass(11, 1, cols=cols, dst=sums[:])
-            for n in range(0, width, P):
-                up_pass(11, sums[:, n : n + P], slice(cols.start + n, cols.start + n + P), stop=(n + P == width))
-            store(11, sums[:], cols=cols)
+            for c in (0, 1, 4):
+                w_pass(acc[i][:], i, c, start=(c == 0), stop=(c == 4))
+            store_tile(i, acc[i][:])
+        for h in range(2):
+            cols = slice(H * h, H * (h + 1))
+            sums = bank(h, [P, H])
+            for c in (0, 1, 4):
+                w_pass(sums[:], 11, c, cols, start=(c == 0), stop=(c == 4))
+            store_tile(11, sums[:], cols=cols)

@@ -16,7 +16,7 @@ FP4X4 = mybir.dt.float4_e2m1fn_x4
 P = 128
 PACK = 4
 H = T // 2
-W8_ROW = 4
+W8_ROW = (4, 8)
 
 
 def tile_mix_three_fm_none_kernel(
@@ -31,35 +31,26 @@ def tile_mix_three_fm_none_kernel(
         def sb(name, shape, dtype):
             return keep.tile(shape, dtype, name=name, align_bytes=256)
 
-        w4_plane = sb("w4_plane", [P, 2, M], U8)
-        w8_plane = sb("w8_plane", [P, 2, M], U8)
+        w4_plane = [sb(f"w4_plane{a}", [P, M], U8) for a in range(2)]
+        w8_plane = [sb(f"w8_plane{a}", [P, M], U8) for a in range(2)]
         up_plane = sb("up_plane", [P, M], U8)
         warm_in = sb("warm_in", [P, 1], F32)
         warm_out = sb("warm_out", [P, 1], F32)
         nc.vector.memset(warm_in[:], 0.0)
-        nc.vector.memset(w4_plane[:].bitcast(I32), 0)
-        nc.vector.memset(w8_plane[:].bitcast(I32), 0)
-        nc.vector.memset(up_plane[:].bitcast(I32), 0)
+        for plane in (*w4_plane, *w8_plane, up_plane):
+            nc.vector.memset(plane[:].bitcast(I32), 0)
         nc.scalar.copy(warm_out[:], warm_in[:])
 
         w8_rows = w8_scales.rearrange("a (q r) n -> r q a n", r=4)
         w4_rows = w4_scales.rearrange("a (q r) n -> r q a n", r=4)
         up_rows = up_scales.rearrange("a (q r) n -> r q a n", r=4)
 
-        def load_rows(queue, plane, rows, a):
+        def load_rows(queue, plane, rows, a, first=0):
             for r in range(4):
-                queue.dma_start(out=plane[r:P:32, :].bitcast(I32), in_=rows[r][:, a, :].bitcast(I32))
-
-        def load_w4_rows(queue):
-            for r in range(4):
-                queue.dma_start(out=w4_plane[r:P:32].bitcast(I32), in_=w4_rows[r].bitcast(I32))
-
-        def load_w8_rows(queue):
-            for r in range(4):
-                queue.dma_start(out=w8_plane[W8_ROW + r : P : 32].bitcast(I32), in_=w8_rows[r].bitcast(I32))
+                queue.dma_start(out=plane[first + r : P : 32, :].bitcast(I32), in_=rows[r][:, a, :].bitcast(I32))
 
         x_raw = {c: sb(f"x_raw{c}", [P, PACK, T], F32) for c in (2, 3, 0)}
-        x_raw_half = [sb(f"x_raw1_{h}", [P, PACK, H], F32) for h in range(2)]
+        last = {a: sb(f"x_raw1_{a}", [P, PACK, b - a], F32) for a, b in ((0, H), (H, T))}
         d_raw = [sb(f"d_raw{c}", [P, PACK, R], F32) for c in range(4)]
         words = {}
         w8_view = w8_words.rearrange("a p n i -> p a (n i)")
@@ -84,23 +75,26 @@ def tile_mix_three_fm_none_kernel(
                 words[c, i] = tile[:, width * (i - first) : width * (i - first + 1)]
 
         load_k(x_raw[2], x, 2)
-        load_k(x_raw[3], x, 3)
-        load_w4_rows(nc.gpsimd)
         load_words(2, 0, 12)
+        load_rows(nc.sync, w4_plane[0], w4_rows, 0)
+        load_rows(nc.gpsimd, w4_plane[1], w4_rows, 1)
+        load_k(x_raw[3], x, 3)
         load_words(3, 0, 12)
-        load_w8_rows(nc.gpsimd)
+        load_rows(nc.gpsimd, w8_plane[0], w8_rows, 0, W8_ROW[0])
+        load_rows(nc.gpsimd, w8_plane[1], w8_rows, 1, W8_ROW[1])
         load_words(0, 4, 8)
         load_k(x_raw[0], x, 0)
         for c in (2, 3, 0, 1):
             load_k(d_raw[c], down, c)
         load_words(0, 0, 4)
-        load_k(x_raw_half[0], x, 1, slice(0, H))
-        load_k(x_raw_half[1], x, 1, slice(H, T))
+        load_k(last[0], x, 1, slice(0, H))
+        load_k(last[H], x, 1, slice(H, T))
         load_words(1, 0, 4)
         load_rows(nc.sync, up_plane, up_rows, 0)
         load_words(4, 0, 12)
         load_words(1, 4, 8)
-        load_w8_both(8, 12)
+        load_words(0, 8, 12)
+        load_words(1, 8, 12)
 
         x_q = [sb(f"x_q{c}", [P, T], U32) for c in range(4)]
         x_s = [sb(f"x_s{c}", [P, T], U8) for c in range(4)]
@@ -141,6 +135,9 @@ def tile_mix_three_fm_none_kernel(
             interleave(on_vector, x_b[c], x_raw[c], 0, share)
             interleave(on_scalar, x_b[c], x_raw[c], share, T)
 
+        def round_last(copy, first, a, b):
+            interleave(copy, x_b[1], last[first], a - first, b - first, first)
+
         def prepare_down(c, share):
             permute(on_vector, d_b[c], d_raw[c], 0, share)
             permute(on_scalar, d_b[c], d_raw[c], share, P)
@@ -153,10 +150,10 @@ def tile_mix_three_fm_none_kernel(
         def w_pass(dst, i, c, cols=slice(0, T), start=False, stop=False):
             tile_cols = slice(P * i, P * (i + 1))
             if c < 2:
-                lhs, lhs_scale = words[c, i].bitcast(FP8X4), w8_plane[W8_ROW:P, c, tile_cols]
+                lhs, lhs_scale = words[c, i].bitcast(FP8X4), w8_plane[c][W8_ROW[c] : P, tile_cols]
             else:
                 lhs = words[c, i].bitcast(FP4X4)
-                lhs_scale = w4_plane[:, c - 2, tile_cols] if c < 4 else up_plane[:, tile_cols]
+                lhs_scale = w4_plane[c - 2][:, tile_cols] if c < 4 else up_plane[:, tile_cols]
             nc.tensor.matmul_mx(
                 out=dst, lhsT=lhs, lhsT_scale=lhs_scale,
                 rhs=x_q[c][:, cols].bitcast(FP8X4), rhs_scale=x_s[c][:, cols], start=start, stop=stop,
@@ -228,14 +225,13 @@ def tile_mix_three_fm_none_kernel(
             acc[8 + n] = bank(n, [P, T])
             acc[n] = bank(4 + n, [P, T])
         for c in (2, 3):
-            round_x(c, 320)
+            round_x(c, 256 if c == 2 else 224)
             quantize_x(c)
-        for c in (2, 3):
             for i in (8, 9, 10, 11, 0, 1, 2, 3):
                 w_pass(acc[i][:], i, c, start=(c == 2), stop=(c == 3 and i >= 8))
         for i in range(8, 12):
             park_tile(i, acc[i], on_scalar if i % 2 == 0 else on_vector)
-        round_x(0, 320)
+        round_x(0, 352)
         quantize_x(0)
         for i in range(4, 8):
             acc[i] = bank(i - 4, [P, T])
@@ -246,7 +242,7 @@ def tile_mix_three_fm_none_kernel(
         prepare_down(2, 100)
         for i in range(4, 8):
             park_tile(i, acc[i], on_scalar)
-        prepare_down(3, 100)
+        prepare_down(3, 108)
         for q in range(4):
             h_acc[q] = bank(q, [P, PACK, P])
         for c in (2, 3):
@@ -259,16 +255,18 @@ def tile_mix_three_fm_none_kernel(
             w_pass(acc[i][:], i, 0)
         prepare_down(1, 76)
 
-        interleave(on_vector, x_b[1], x_raw_half[0], 0, P)
-        interleave(on_vector, x_b[1], x_raw_half[0], P, P + 32)
-        interleave(on_scalar, x_b[1], x_raw_half[0], P + 32, H)
+        round_last(on_vector, 0, 0, P)
+        round_last(on_vector, 0, P, P + 32)
+        round_last(on_scalar, 0, P + 32, H)
         for q in range(2):
             quantize_x(1, P * q, P * (q + 1))
             h_passes(q, 1)
-        interleave(on_vector, x_b[1], x_raw_half[1], 0, 88, H)
-        interleave(on_scalar, x_b[1], x_raw_half[1], 88, P, H)
-        interleave(on_vector, x_b[1], x_raw_half[1], P, P + 80, H)
-        interleave(on_scalar, x_b[1], x_raw_half[1], P + 80, H, H)
+        round_last(on_vector, H, H + 0, H + 88)
+        round_last(on_scalar, H, H + 88, H + P)
+        round_last(on_vector, H, H + P, H + P + 80)
+        round_last(on_scalar, H, H + P + 80, H + H)
+        for i in (0, 1):
+            w_pass(acc[i][:, :H], i, 1, slice(0, H))
         for q in (2, 3):
             quantize_x(1, P * q, P * (q + 1))
             h_passes(q, 1)
@@ -280,33 +278,34 @@ def tile_mix_three_fm_none_kernel(
         for q in range(1, 4):
             quantize_x(4, P * q, P * (q + 1))
 
-        for i in range(4):
+        for i in (0, 1):
+            w_pass(acc[i][:, H:], i, 1, slice(H, T))
+        for i in (2, 3):
             w_pass(acc[i][:], i, 1)
         for q in range(4):
             cols = slice(P * q, P * (q + 1))
+            if q == 3:
+                acc[4] = bank(0, [P, T])
+                w_pass(acc[4][:], 4, 1, start=True)
             w_pass(acc[0][:, cols], 0, 4, cols, stop=(q == 3))
         for h in range(2):
             cols = slice(H * h, H * (h + 1))
             store_tile(0, acc[0][:, cols], on_scalar, cols)
-        w_pass(acc[1][:], 1, 4, stop=True)
-        store_tile(1, acc[1][:], on_vector)
-        for first in (2, 4, 6):
-            res = sb(f"res{first}", [P, 2, T], F32)
-            for i in (first, first + 1):
-                if i >= 4:
-                    acc[i] = bank(i - 4, [P, T])
-                    w_pass(acc[i][:], i, 1, start=True)
-                w_pass(acc[i][:], i, 4, stop=True)
-                drain(res[:, i - first, :], i, acc[i][:], on_scalar)
-            store_group(first, res)
-        for i in range(8, 11):
+        for i in range(1, 4):
+            w_pass(acc[i][:], i, 4, stop=True)
+            store_tile(i, acc[i][:], on_vector if i == 1 else on_scalar)
+        w_pass(acc[4][:], 4, 4, stop=True)
+        store_tile(4, acc[4][:])
+        for i in range(5, 10):
             acc[i] = bank(i - 4, [P, T])
-            for c in (0, 1, 4):
-                w_pass(acc[i][:], i, c, start=(c == 0), stop=(c == 4))
+            chunks = (1, 4) if i < 8 else (0, 1, 4)
+            for c in chunks:
+                w_pass(acc[i][:], i, c, start=(c == chunks[0]), stop=(c == 4))
             store_tile(i, acc[i][:])
-        for h in range(2):
-            cols = slice(H * h, H * (h + 1))
-            sums = bank(h, [P, H])
-            for c in (0, 1, 4):
-                w_pass(sums[:], 11, c, cols, start=(c == 0), stop=(c == 4))
-            store_tile(11, sums[:], cols=cols)
+        for i in range(10, 12):
+            for h in range(2):
+                cols = slice(H * h, H * (h + 1))
+                sums = bank(2 * (i - 10) + h, [P, H])
+                for c in (0, 1, 4):
+                    w_pass(sums[:], i, c, cols, start=(c == 0), stop=(c == 4))
+                store_tile(i, sums[:], cols=cols)

@@ -37,7 +37,7 @@ def tile_mix_three_fm_none_kernel(
         warm_in = sb("warm_in", [P, 1], F32)
         warm_out = sb("warm_out", [P, 1], F32)
         nc.vector.memset(warm_in[:], 0.0)
-        for plane in (*w4_plane, *w8_plane, up_plane):
+        for plane in (w4_plane[1], w8_plane[0], w4_plane[0], w8_plane[1], up_plane):
             nc.vector.memset(plane[:].bitcast(I32), 0)
         nc.scalar.copy(warm_out[:], warm_in[:])
 
@@ -81,7 +81,6 @@ def tile_mix_three_fm_none_kernel(
         load_k(x_raw[3], x, 3)
         load_words(3, 0, 12)
         load_rows(nc.gpsimd, w8_plane[0], w8_rows, 0, W8_ROW[0])
-        load_rows(nc.gpsimd, w8_plane[1], w8_rows, 1, W8_ROW[1])
         load_words(0, 4, 8)
         load_k(x_raw[0], x, 0)
         for c in (2, 3, 0, 1):
@@ -89,12 +88,12 @@ def tile_mix_three_fm_none_kernel(
         load_words(0, 0, 4)
         load_k(last[0], x, 1, slice(0, H))
         load_k(last[H], x, 1, slice(H, T))
-        load_words(1, 0, 4)
+        load_rows(nc.sync, w8_plane[1], w8_rows, 1, W8_ROW[1])
+        load_words(1, 0, 6)
         load_rows(nc.sync, up_plane, up_rows, 0)
         load_words(4, 0, 12)
-        load_words(1, 4, 8)
+        load_words(1, 6, 12)
         load_words(0, 8, 12)
-        load_words(1, 8, 12)
 
         x_q = [sb(f"x_q{c}", [P, T], U32) for c in range(4)]
         x_s = [sb(f"x_s{c}", [P, T], U8) for c in range(4)]
@@ -265,8 +264,6 @@ def tile_mix_three_fm_none_kernel(
         round_last(on_scalar, H, H + 88, H + P)
         round_last(on_vector, H, H + P, H + P + 80)
         round_last(on_scalar, H, H + P + 80, H + H)
-        for i in (0, 1):
-            w_pass(acc[i][:, :H], i, 1, slice(0, H))
         for q in (2, 3):
             quantize_x(1, P * q, P * (q + 1))
             h_passes(q, 1)
@@ -278,13 +275,11 @@ def tile_mix_three_fm_none_kernel(
         for q in range(1, 4):
             quantize_x(4, P * q, P * (q + 1))
 
-        for i in (0, 1):
-            w_pass(acc[i][:, H:], i, 1, slice(H, T))
-        for i in (2, 3):
+        for i in range(4):
             w_pass(acc[i][:], i, 1)
         for q in range(4):
             cols = slice(P * q, P * (q + 1))
-            if q == 3:
+            if q == 0:
                 acc[4] = bank(0, [P, T])
                 w_pass(acc[4][:], 4, 1, start=True)
             w_pass(acc[0][:, cols], 0, 4, cols, stop=(q == 3))
@@ -296,16 +291,16 @@ def tile_mix_three_fm_none_kernel(
             store_tile(i, acc[i][:], on_vector if i == 1 else on_scalar)
         w_pass(acc[4][:], 4, 4, stop=True)
         store_tile(4, acc[4][:])
-        for i in range(5, 10):
+        for i in range(5, 11):
             acc[i] = bank(i - 4, [P, T])
             chunks = (1, 4) if i < 8 else (0, 1, 4)
             for c in chunks:
                 w_pass(acc[i][:], i, c, start=(c == chunks[0]), stop=(c == 4))
             store_tile(i, acc[i][:])
-        for i in range(10, 12):
+        for i in range(11, 12):
             for h in range(2):
                 cols = slice(H * h, H * (h + 1))
-                sums = bank(2 * (i - 10) + h, [P, H])
+                sums = bank(h, [P, H])
                 for c in (0, 1, 4):
                     w_pass(sums[:], i, c, cols, start=(c == 0), stop=(c == 4))
                 store_tile(i, sums[:], cols=cols)

@@ -37,7 +37,8 @@ def tile_mix_three_fm_none_kernel(
         warm_in = sb("warm_in", [P, 1], F32)
         warm_out = sb("warm_out", [P, 1], F32)
         nc.vector.memset(warm_in[:], 0.0)
-        for plane in (w4_plane[1], w8_plane[0], w4_plane[0], w8_plane[1], up_plane):
+        nc.gpsimd.memset(w4_plane[1][:].bitcast(I32), 0)
+        for plane in (w4_plane[0], *w8_plane):
             nc.vector.memset(plane[:].bitcast(I32), 0)
         nc.scalar.copy(warm_out[:], warm_in[:])
 
@@ -81,6 +82,7 @@ def tile_mix_three_fm_none_kernel(
         load_k(x_raw[3], x, 3)
         load_words(3, 0, 12)
         load_rows(nc.gpsimd, w8_plane[0], w8_rows, 0, W8_ROW[0])
+        load_rows(nc.gpsimd, w8_plane[1], w8_rows, 1, W8_ROW[1])
         load_words(0, 4, 8)
         load_k(x_raw[0], x, 0)
         for c in (2, 3, 0, 1):
@@ -88,12 +90,7 @@ def tile_mix_three_fm_none_kernel(
         load_words(0, 0, 4)
         load_k(last[0], x, 1, slice(0, H))
         load_k(last[H], x, 1, slice(H, T))
-        load_rows(nc.sync, w8_plane[1], w8_rows, 1, W8_ROW[1])
-        load_words(1, 0, 6)
-        load_rows(nc.sync, up_plane, up_rows, 0)
-        load_words(4, 0, 12)
-        load_words(1, 6, 12)
-        load_words(0, 8, 12)
+        load_words(1, 0, 4)
 
         x_q = [sb(f"x_q{c}", [P, T], U32) for c in range(4)]
         x_s = [sb(f"x_s{c}", [P, T], U8) for c in range(4)]
@@ -232,6 +229,12 @@ def tile_mix_three_fm_none_kernel(
             park_tile(i, acc[i], on_scalar if i % 2 == 0 else on_vector)
         round_x(0, 352)
         quantize_x(0)
+        nc.vector.memset(up_plane[:].bitcast(I32), 0)
+        load_rows(nc.sync, up_plane, up_rows, 0)
+        load_words(4, 0, 12)
+        load_words(1, 4, 8)
+        load_words(0, 8, 12)
+        load_words(1, 8, 12)
         for i in range(4, 8):
             acc[i] = bank(i - 4, [P, T])
             w_pass(acc[i][:], i, 2, start=True)
@@ -279,7 +282,7 @@ def tile_mix_three_fm_none_kernel(
             w_pass(acc[i][:], i, 1)
         for q in range(4):
             cols = slice(P * q, P * (q + 1))
-            if q == 0:
+            if q == 3:
                 acc[4] = bank(0, [P, T])
                 w_pass(acc[4][:], 4, 1, start=True)
             w_pass(acc[0][:, cols], 0, 4, cols, stop=(q == 3))

from contextlib import ExitStack

import concourse.mybir as mybir

K, T, R, M = 2048, 512, 512, 1536
FLOPS = 2 * (K * R * T + K * M * T + R * M * T)

F32 = mybir.dt.float32
BF16 = mybir.dt.bfloat16
I32 = mybir.dt.int32
U32 = mybir.dt.uint32
U8 = mybir.dt.uint8
FP8X4 = mybir.dt.float8_e4m3fn_x4
FP4X4 = mybir.dt.float4_e2m1fn_x4

P = 128
PACK = 4
H = T // 2
W8_ROW = (4, 8)


def tile_mix_three_fm_none_kernel(
    tc, x, w8_words, w8_scales, w4_words, w4_scales, down, up_words, up_scales, out
):
    nc = tc.nc
    with ExitStack() as ctx:
        keep = ctx.enter_context(tc.tile_pool(name="keep", bufs=1))
        psum = ctx.enter_context(tc.psum_pool(name="psum", bufs=1))
        ctx.enter_context(tc.manual_schedule())

        def sb(name, shape, dtype):
            return keep.tile(shape, dtype, name=name, align_bytes=256)

        w4_plane = [sb(f"w4_plane{a}", [P, M], U8) for a in range(2)]
        w8_plane = [sb(f"w8_plane{a}", [P, M], U8) for a in range(2)]
        up_plane = sb("up_plane", [P, M], U8)
        warm_in = sb("warm_in", [P, 1], F32)
        warm_out = sb("warm_out", [P, 1], F32)
        nc.vector.memset(warm_in[:], 0.0)
        nc.gpsimd.memset(w4_plane[1][:].bitcast(I32), 0)
        for plane in (w4_plane[0], *w8_plane):
            nc.vector.memset(plane[:].bitcast(I32), 0)
        nc.scalar.copy(warm_out[:], warm_in[:])

        w8_rows = w8_scales.rearrange("a (q r) n -> r q a n", r=4)
        w4_rows = w4_scales.rearrange("a (q r) n -> r q a n", r=4)
        up_rows = up_scales.rearrange("a (q r) n -> r q a n", r=4)

        def load_rows(queue, plane, rows, a, first=0):
            for r in range(4):
                queue.dma_start(out=plane[first + r : P : 32, :].bitcast(I32), in_=rows[r][:, a, :].bitcast(I32))

        x_raw = {c: sb(f"x_raw{c}", [P, PACK, T], F32) for c in (2, 3, 0)}
        last = {a: sb(f"x_raw1_{a}", [P, PACK, b - a], F32) for a, b in ((0, H), (H, T))}
        d_raw = [sb(f"d_raw{c}", [P, PACK, R], F32) for c in range(4)]
        words = {}
        w8_view = w8_words.rearrange("a p n i -> p a (n i)")

        def load_k(tile, src, c, cols=slice(0, T)):
            rows = src[512 * c : 512 * (c + 1), cols].rearrange("(p j) w -> p j w", j=PACK)
            nc.sync.dma_start(out=tile[:], in_=rows)

        def load_w8_both(first, last):
            tile = sb(f"words8_{first}", [P, 2, 4 * P * (last - first)], U8)
            nc.sync.dma_start(out=tile[:].bitcast(I32), in_=w8_view[:, :, 4 * P * first : 4 * P * last].bitcast(I32))
            for c in range(2):
                for i in range(first, last):
                    words[c, i] = tile[:, c, 4 * P * (i - first) : 4 * P * (i - first + 1)]

        def load_words(c, first, last):
            width = 4 * P if c < 2 else 2 * P
            src = w8_view[:, c, :] if c < 2 else w4_words[c - 2] if c < 4 else up_words[0]
            tile = sb(f"words{c}_{first}", [P, width * (last - first)], U8)
            nc.sync.dma_start(out=tile[:].bitcast(I32), in_=src[:, width * first : width * last].bitcast(I32))
            for i in range(first, last):
                words[c, i] = tile[:, width * (i - first) : width * (i - first + 1)]

        load_k(x_raw[2], x, 2)
        load_words(2, 0, 12)
        load_rows(nc.sync, w4_plane[0], w4_rows, 0)
        load_rows(nc.gpsimd, w4_plane[1], w4_rows, 1)
        load_k(x_raw[3], x, 3)
        load_words(3, 0, 12)
        load_rows(nc.gpsimd, w8_plane[0], w8_rows, 0, W8_ROW[0])
        load_rows(nc.gpsimd, w8_plane[1], w8_rows, 1, W8_ROW[1])
        load_words(0, 4, 8)
        load_k(x_raw[0], x, 0)
        for c in (2, 3, 0, 1):
            load_k(d_raw[c], down, c)
        load_words(0, 0, 4)
        load_k(last[0], x, 1, slice(0, H))
        load_k(last[H], x, 1, slice(H, T))
        load_words(1, 0, 4)

        x_q = [sb(f"x_q{c}", [P, T], U32) for c in range(4)]
        x_s = [sb(f"x_s{c}", [P, T], U8) for c in range(4)]
        x_b = [sb(f"x_b{c}", [P, PACK * T], BF16) for c in range(4)]
        d_q = [sb(f"d_q{c}", [P, R], U32) for c in range(4)]
        d_s = [sb(f"d_s{c}", [P, R], U8) for c in range(4)]
        d_b = [sb(f"d_b{c}", [P, PACK * R], BF16) for c in range(4)]
        h_b = sb("h_b", [P, PACK * T], BF16)
        x_q.append(sb("h_q", [P, T], U32))
        x_s.append(sb("h_s", [P, T], U8))
        x_b.append(h_b)
        part = {}
        on_vector = nc.vector.tensor_copy
        on_scalar = nc.scalar.copy

        def interleave(copy, dst, raw, a, b, first=0):
            copy(
                dst[:, PACK * (first + a) : PACK * (first + b)].rearrange("p (c i t) -> p c t i", i=4, t=4),
                raw[:, :, a:b].rearrange("p t (c i) -> p c t i", i=4),
            )

        def permute(copy, dst, raw, a, b):
            for u in range(2):
                copy(
                    dst[:].rearrange("p (u e m j) -> p u m j e", u=2, e=2, j=4)[:, u, a:b],
                    raw[:].rearrange("p j (m u e) -> p u m j e", u=2, e=2)[:, u, a:b],
                )

        def quantize(codes, scales, values, a, b):
            nc.vector.quantize_mx(
                out=codes[:, a:b].bitcast(FP8X4), scales=scales[:, a:b], in_=values[:, PACK * a : PACK * b]
            )

        def quantize_x(c, a=0, b=T):
            quantize(x_q[c], x_s[c], x_b[c], a, b)

        def round_x(c, share):
            interleave(on_vector, x_b[c], x_raw[c], 0, share)
            interleave(on_scalar, x_b[c], x_raw[c], share, T)

        def round_last(copy, first, a, b):
            interleave(copy, x_b[1], last[first], a - first, b - first, first)

        def prepare_down(c, share):
            permute(on_vector, d_b[c], d_raw[c], 0, share)
            permute(on_scalar, d_b[c], d_raw[c], share, P)
            for u in range(2):
                quantize(d_q[c], d_s[c], d_b[c], R // 2 * u, R // 2 * (u + 1))

        def bank(b, shape):
            return psum.tile(shape, F32, name=f"bank{b}")

        def w_pass(dst, i, c, cols=slice(0, T), start=False, stop=False):
            tile_cols = slice(P * i, P * (i + 1))
            if c < 2:
                lhs, lhs_scale = words[c, i].bitcast(FP8X4), w8_plane[c][W8_ROW[c] : P, tile_cols]
            else:
                lhs = words[c, i].bitcast(FP4X4)
                lhs_scale = w4_plane[c - 2][:, tile_cols] if c < 4 else up_plane[:, tile_cols]
            nc.tensor.matmul_mx(
                out=dst, lhsT=lhs, lhsT_scale=lhs_scale,
                rhs=x_q[c][:, cols].bitcast(FP8X4), rhs_scale=x_s[c][:, cols], start=start, stop=stop,
            )

        def half_passes(sums, g, h, c, start=False, stop=False):
            for e in range(2):
                w_pass(sums[:, e, :], 2 * g + e, c, slice(H * h, H * (h + 1)), start and e == 0, stop and e == 1)

        def park(key, sums, copy):
            part[key] = sb(f"part{key[0]}_{key[1]}", [P, 2, H], F32)
            copy(part[key][:], sums[:])

        def park_tile(i, sums, copy):
            g = i // 2
            if (g, 0) not in part:
                both = sb(f"part{g}", [P, 2, T], F32)
                for h in range(2):
                    part[g, h] = both[:, :, H * h : H * (h + 1)]
                part[g] = both
            copy(part[g][:, i % 2, :], sums[:])

        h_acc = {}

        def h_passes(q, c):
            cols = slice(P * q, P * (q + 1))
            for t in range(4):
                rows = slice(P * t, P * (t + 1))
                nc.tensor.matmul_mx(
                    out=h_acc[q][:, t, :], lhsT=d_q[c][:, rows].bitcast(FP8X4), lhsT_scale=d_s[c][:, rows],
                    rhs=x_q[c][:, cols].bitcast(FP8X4), rhs_scale=x_s[c][:, cols],
                    start=(c == 2 and t == 0), stop=(c == 1 and t == 3),
                )

        def h_out(copy, q):
            copy(
                h_b[:, PACK * P * q : PACK * P * (q + 1)].rearrange("p (m e t) -> p m t e", e=2, t=4),
                h_acc[q][:].rearrange("p t (m e) -> p m t e", e=2),
            )

        out_pairs = out.rearrange("(g e p) t -> g p e t", e=2, p=P)

        def store_half_pair(g, h, sums, copy=None):
            cols = slice(H * h, H * (h + 1))
            res = sb(f"res_pair{g}_{h}", [P, 2, H], F32)
            if (g, h) in part:
                nc.vector.tensor_add(res[:], sums[:], part[g, h][:])
            else:
                copy(res[:], sums[:])
            nc.sync.dma_start(out=out_pairs[g][:, :, cols], in_=res[:])

        def drain(res, i, sums, copy=None, cols=slice(0, T)):
            if i // 2 in part:
                nc.vector.tensor_add(res, sums, part[i // 2][:, i % 2, cols])
            else:
                copy(res, sums)

        def store_tile(i, sums, copy=None, cols=slice(0, T)):
            res = sb(f"res{i}_{cols.start}", [P, cols.stop - cols.start], F32)
            drain(res[:], i, sums, copy, cols)
            nc.sync.dma_start(out=out[P * i : P * (i + 1), cols], in_=res[:])

        def store_group(first, res):
            rows = out[P * first : P * (first + res.shape[1]), :].rearrange("(e p) t -> p e t", p=P)
            nc.sync.dma_start(out=rows, in_=res[:])

        acc = {}
        for n in range(4):
            acc[8 + n] = bank(n, [P, T])
            acc[n] = bank(4 + n, [P, T])
        for c in (2, 3):
            round_x(c, 256 if c == 2 else 224)
            quantize_x(c)
            for i in (8, 9, 10, 11, 0, 1, 2, 3):
                w_pass(acc[i][:], i, c, start=(c == 2), stop=(c == 3 and i >= 8))
        for i in range(8, 12):
            park_tile(i, acc[i], on_scalar if i % 2 == 0 else on_vector)
        round_x(0, 352)
        quantize_x(0)
        nc.vector.memset(up_plane[:].bitcast(I32), 0)
        load_rows(nc.sync, up_plane, up_rows, 0)
        load_words(4, 0, 12)
        load_words(1, 4, 8)
        load_words(0, 8, 12)
        load_words(1, 8, 12)
        for i in range(4, 8):
            acc[i] = bank(i - 4, [P, T])
            w_pass(acc[i][:], i, 2, start=True)
            w_pass(acc[i][:], i, 3)
        for i in range(4, 8):
            w_pass(acc[i][:], i, 0, stop=True)
        prepare_down(2, 100)
        for i in range(4, 8):
            park_tile(i, acc[i], on_scalar)
        prepare_down(3, 108)
        for q in range(4):
            h_acc[q] = bank(q, [P, PACK, P])
        for c in (2, 3):
            for q in range(4):
                h_passes(q, c)
        prepare_down(0, 76)
        for q in range(4):
            h_passes(q, 0)
        for i in range(4):
            w_pass(acc[i][:], i, 0)
        prepare_down(1, 76)

        round_last(on_vector, 0, 0, P)
        round_last(on_vector, 0, P, P + 32)
        round_last(on_scalar, 0, P + 32, H)
        for q in range(2):
            quantize_x(1, P * q, P * (q + 1))
            h_passes(q, 1)
        round_last(on_vector, H, H + 0, H + 88)
        round_last(on_scalar, H, H + 88, H + P)
        round_last(on_vector, H, H + P, H + P + 80)
        round_last(on_scalar, H, H + P + 80, H + H)
        for q in (2, 3):
            quantize_x(1, P * q, P * (q + 1))
            h_passes(q, 1)
        h_out(on_scalar, 0)
        h_out(on_scalar, 1)
        quantize_x(4, 0, P)
        h_out(on_vector, 2)
        h_out(on_scalar, 3)
        for q in range(1, 4):
            quantize_x(4, P * q, P * (q + 1))

        for i in range(4):
            w_pass(acc[i][:], i, 1)
        for q in range(4):
            cols = slice(P * q, P * (q + 1))
            if q == 3:
                acc[4] = bank(0, [P, T])
                w_pass(acc[4][:], 4, 1, start=True)
            w_pass(acc[0][:, cols], 0, 4, cols, stop=(q == 3))
        for h in range(2):
            cols = slice(H * h, H * (h + 1))
            store_tile(0, acc[0][:, cols], on_scalar, cols)
        for i in range(1, 4):
            w_pass(acc[i][:], i, 4, stop=True)
            store_tile(i, acc[i][:], on_vector if i == 1 else on_scalar)
        w_pass(acc[4][:], 4, 4, stop=True)
        store_tile(4, acc[4][:])
        for i in range(5, 11):
            acc[i] = bank(i - 4, [P, T])
            chunks = (1, 4) if i < 8 else (0, 1, 4)
            for c in chunks:
                w_pass(acc[i][:], i, c, start=(c == chunks[0]), stop=(c == 4))
            store_tile(i, acc[i][:])
        for i in range(11, 12):
            for h in range(2):
                cols = slice(H * h, H * (h + 1))
                sums = bank(h, [P, H])
                for c in (0, 1, 4):
                    w_pass(sums[:], i, c, cols, start=(c == 0), stop=(c == 4))
                store_tile(i, sums[:], cols=cols)
